import numpy as np
import ml_dtypes


def mxq(x, axis, fmt="e4m3"):
    dtype, down = {"e4m3": (ml_dtypes.float8_e4m3fn, 7), "e5m2": (ml_dtypes.float8_e5m2, 14)}[fmt]
    v = np.moveaxis(np.asarray(x, np.float32).astype(ml_dtypes.bfloat16).astype(np.float64), axis, -1)
    blocks = v.reshape(v.shape[:-1] + (-1, 32))
    amax = np.abs(blocks).max(-1, keepdims=True)
    byte = np.maximum(np.where(amax > 0, np.frexp(amax)[1] - 1 + 127, 0) - down, 1)
    scale = np.exp2(byte - 127.0)
    codes = (blocks / scale).astype(np.float32).astype(dtype).astype(np.float64)
    return np.moveaxis((codes * scale).reshape(v.shape), -1, axis)


WIDE = False


def mx_kscale(k):
    if not WIDE:
        return np.ones(k)
    levels = np.array([10, -10, 5, -5, 0])
    if k % 512:
        return np.exp2(np.random.permutation(np.resize(levels, k // 32))).repeat(32)
    a = np.empty((k // 512, 16))
    for p in range(k // 512):
        a[p, :8] = np.random.permutation(np.resize(levels, 8))
        for g in range(8):
            far = levels[np.abs(levels - a[p, g]) >= 10]
            a[p, g + 8] = far[np.random.randint(len(far))]
    return np.exp2(a.ravel()).repeat(32)


def f64(x):
    return np.asarray(x).astype(np.float64)


def striped(idx):
    return np.tile(idx.reshape(-1, 16).T, (8, 1)).astype(np.uint16)


def unstriped(offs):
    return offs[:16].T.reshape(-1).astype(np.int64)


E2M1 = np.array([0.0, 0.5, 1.0, 1.5, 2.0, 3.0, 4.0, 6.0, -0.0, -0.5, -1.0, -1.5, -2.0, -3.0, -4.0, -6.0])


def pack_weight(w, fmt):
    k, n = w.shape
    w = f64(np.asarray(w, np.float32).astype(ml_dtypes.bfloat16)).reshape(k // 32, 32, n)
    amax = np.abs(w).max(1)
    if fmt == "e4m3":
        byte = np.frexp(amax)[1] - 1 + 127 - 7
    else:
        mant, ex = np.frexp(amax / 6.0)
        byte = np.where(mant > 0.5, ex, ex - 1) + 127
    byte = np.clip(np.where(amax > 0, byte, 1), 1, 254)
    scaled = (w * np.exp2(127.0 - byte)[:, None, :]).reshape(k, n).astype(np.float32)
    by_word = np.ascontiguousarray(scaled.reshape(k // 512, 128, 4, n).transpose(0, 1, 3, 2))
    if fmt == "e4m3":
        words = by_word.astype(ml_dtypes.float8_e4m3fn).view(np.uint8)
    else:
        c = by_word.astype(ml_dtypes.float4_e2m1fn).view(np.uint8) & 0xF
        words = (c[..., 0::2] | (c[..., 1::2] << 4)).reshape(k // 512, 128, 2 * n)
    return np.ascontiguousarray(words), np.ascontiguousarray(byte.astype(np.uint8).reshape(k // 512, 16, n))


def unpack_weight(words, scales, fmt):
    g, _, n = scales.shape
    words = np.ascontiguousarray(words).reshape(g, 128, n, -1)
    if fmt == "e4m3":
        vals = words.view(ml_dtypes.float8_e4m3fn).astype(np.float64)
    else:
        nib = np.empty((g, 128, n, 4), np.uint8)
        nib[..., 0::2] = words & 0xF
        nib[..., 1::2] = words >> 4
        vals = E2M1[nib]
    vals = vals * np.repeat(np.exp2(scales.astype(np.float64) - 127.0), 8, axis=1)[..., None]
    return vals.transpose(0, 1, 3, 2).reshape(g * 512, n)


def gelu(v):
    return 0.5 * v * (1.0 + np.tanh(np.sqrt(2.0 / np.pi) * (v + 0.044715 * v**3)))


def striped8(idx):
    return np.concatenate([v.reshape(-1, 16).T for v in idx]).astype(np.uint16)


def unstriped8(offs):
    return np.stack([offs[16 * g:16 * g + 16].T.reshape(-1) for g in range(8)]).astype(np.int64)


def runs(v, idx8):
    k = np.arange(v.shape[0])
    return v[k[:, None], idx8[k % 512 // 64]]


K, T, S, P, H, N = 512, 2048, 1024, 512, 1024, 384


def setup_inputs():
    n = np.random.standard_normal
    s = mx_kscale(K)[:, None]
    u = mx_kscale(H)[:, None]
    d = {}
    d["tab_words"], d["tab_scales"] = pack_weight(n((K, T)) * s, "e4m3")
    d["offs"] = striped8(np.stack([np.random.permutation(T)[:S] for _ in range(8)]))
    d["wa"] = (n((K, H)) / s / K ** 0.5 * u.T).astype(np.float32)
    d["wb_words"], d["wb_scales"] = pack_weight(n((K, H)) / s / K ** 0.5 * u.T, "e2m1")
    d["wd_words"], d["wd_scales"] = pack_weight(n((K, H)) / s / K ** 0.5, "e4m3")
    d["pos1"] = striped(np.random.permutation(S)[:P])
    d["pos2"] = striped(np.random.permutation(S)[:P])
    d["w2"] = (1.3 * n((H, N)) / u / H ** 0.5).astype(np.float32)
    d["theta"] = (0.8 * n(N)).astype(np.float32)
    return d


def reference(tab_words, tab_scales, offs, wa, wb_words, wb_scales, wd_words, wd_scales, pos1, pos2, w2, theta):
    v = runs(unpack_weight(tab_words, tab_scales, "e4m3"), unstriped8(offs))
    a = mxq(f64(wa), 0, "e4m3").T @ v
    b = unpack_weight(wb_words, wb_scales, "e2m1").T @ v
    d = unpack_weight(wd_words, wd_scales, "e4m3").T @ v
    h = a + b * d
    z = h[:, unstriped(pos1)] - h[:, unstriped(pos2)]
    zq = mxq(z, 0, "e4m3")
    y = mxq(f64(w2), 0, "e4m3").T @ zq
    out = 1.0 / (1.0 + np.exp(f64(theta)[:, None] - y))
    return out

@@ -1,0 +1,247 @@
+from contextlib import ExitStack
+
+import concourse.mybir as mybir
+
+K, T, S, NPAIR, H, N = 512, 2048, 1024, 512, 1024, 384
+FLOPS = 3 * 2 * K * H * S + 2 * H * N * NPAIR
+
+F32 = mybir.dt.float32
+BF16 = mybir.dt.bfloat16
+I32 = mybir.dt.int32
+U32 = mybir.dt.uint32
+U16 = mybir.dt.uint16
+U8 = mybir.dt.uint8
+FP8X4 = mybir.dt.float8_e4m3fn_x4
+FP4X4 = mybir.dt.float4_e2m1fn_x4
+ALU = mybir.AluOpType
+ACT = mybir.ActivationFunctionType
+
+P = 128
+PACK = 4
+BANK = 512
+PASSES = H // (P * PACK)
+NT = N // P
+HALF = NPAIR // 2
+
+
+def tile_list_sleep_arousal_scores_kernel(
+    tc, tab_words, tab_scales, offs, wa, wb_words, wb_scales, wd_words, wd_scales, pos1, pos2, w2, theta, out
+):
+    nc = tc.nc
+    with ExitStack() as ctx:
+        keep = ctx.enter_context(tc.tile_pool(name="keep", bufs=1))
+        ring = ctx.enter_context(tc.tile_pool(name="ring", bufs=2))
+        psum = ctx.enter_context(tc.psum_pool(name="psum", bufs=1))
+
+        offs_sb = keep.tile([P, S // 16], U16, name="offs_sb")
+        pos1_sb = keep.tile([P, NPAIR // 16], U16, name="pos1_sb")
+        pos2_sb = keep.tile([P, NPAIR // 16], U16, name="pos2_sb")
+
+        tabs_sb = keep.tile([P, T], U8, name="tabs_sb", align_bytes=64)
+        tabw_sb = keep.tile([P, T], I32, name="tabw_sb", align_bytes=64)
+        ws_raw = keep.tile([P, H], U8, name="ws_raw", tag="raw0", align_bytes=64)
+        vs = keep.tile([P, S], U8, name="vs", align_bytes=64)
+        wb_raw = keep.tile([P, 2 * H], U8, name="wb_raw", align_bytes=64)
+        wd_raw = keep.tile([P, H], I32, name="wd_raw", align_bytes=64)
+
+        nc.vector.memset(vs[:].bitcast(I32), 0)
+
+        nc.sync.dma_start(tabs_sb[:].bitcast(I32), tab_scales[0].bitcast(I32).unsqueeze(1).broadcast_to([16, 8, T // 4]))
+        nc.sync.dma_start(offs_sb[:], offs)
+        nc.sync.dma_start(tabw_sb[:], tab_words[0].rearrange("p t i -> p (t i)").bitcast(I32))
+        for r in range(4):
+            nc.scalar.dma_start(ws_raw[r:P:8, :].bitcast(I32), wb_scales[0, r:16:4, :].bitcast(I32).unsqueeze(1).broadcast_to([4, 4, H // 4]))
+        nc.sync.dma_start(wb_raw[:].bitcast(I32), wb_words[0].bitcast(I32))
+        nc.sync.dma_start(wd_raw[:], wd_words[0].rearrange("p c i -> p (c i)").bitcast(I32))
+        for r in range(4):
+            nc.gpsimd.dma_start(ws_raw[4 + r : P : 8, :].bitcast(I32), wd_scales[0, r:16:4, :].bitcast(I32).unsqueeze(1).broadcast_to([4, 4, H // 4]))
+        wa_rows = wa.rearrange("(p j) c -> p j c", j=PACK)
+        wa_raw = {}
+
+        def load_wa(b):
+            wa_raw[b] = keep.tile([P, PACK, 512], F32, name="wa_raw", tag="wa_raw")
+            nc.sync.dma_start(wa_raw[b][:], wa_rows[:, :, b * 512 : (b + 1) * 512])
+
+        load_wa(0)
+        nc.sync.dma_start(pos1_sb[:], pos1)
+        nc.sync.dma_start(pos2_sb[:], pos2)
+
+        vs_picked = keep.tile([P, S], U8, name="vs_picked", align_bytes=64)
+        nc.vector.tensor_copy(vs_picked[:], tabs_sb[:].indirect(offs_sb[:]))
+        for r in range(4):
+            nc.scalar.dma_start(vs[32 * r : 32 * r + 4, :].bitcast(I32), vs_picked[32 * r : 32 * r + 32 : 8, :].bitcast(I32))
+        vw = []
+        for half in range(2):
+            vw.append(keep.tile([P, BANK], U32, name="vw%d" % half, align_bytes=64))
+            nc.vector.tensor_copy(
+                vw[half][:], tabw_sb[:].bitcast(U32).indirect(offs_sb[:, half * 32 : (half + 1) * 32])
+            )
+
+        theta_sb = keep.tile([P, NT], F32, name="theta_sb")
+        with nc.allow_non_contiguous_dma(reason="one threshold a partition"):
+            nc.gpsimd.dma_start(theta_sb[:], theta.rearrange("(c p) -> p c", p=P))
+        neg_theta = keep.tile([P, NT], F32, name="neg_theta")
+        nc.gpsimd.tensor_scalar(neg_theta[:], theta_sb[:], -1.0, 0.0, ALU.mult, ALU.add)
+
+        ws = keep.tile([P, H], U8, name="ws", align_bytes=64)
+        nc.vector.tensor_copy(
+            ws[:].bitcast(I32).rearrange("p (b t u) -> p b t u", b=PASSES, t=PACK),
+            ws_raw[:].bitcast(I32).rearrange("p (b u t) -> p b t u", b=PASSES, t=PACK),
+        )
+        wb = keep.tile([P, 2 * H], U8, name="wb", align_bytes=64)
+        nc.vector.tensor_copy(
+            wb[:].bitcast(I32).rearrange("p (b t u i) -> p b u t i", b=PASSES, t=PACK, i=2),
+            wb_raw[:].bitcast(I32).rearrange("p (b u t i) -> p b u t i", b=PASSES, t=PACK, i=2),
+        )
+        wd = keep.tile([P, H], I32, name="wd", align_bytes=64)
+        nc.vector.tensor_copy(
+            wd[:].rearrange("p (b t u i) -> p b u t i", b=PASSES, t=PACK, i=4),
+            wd_raw[:].rearrange("p (b u t i) -> p b u t i", b=PASSES, t=PACK, i=4),
+        )
+
+        wa_codes = {}
+        wa_scales = {}
+
+        def cast_wa(j):
+            b, t = divmod(j, PACK)
+            if j == 0:
+                grouped = keep.tile([P, P * PACK], BF16, name="wa_bf0", tag="raw1", align_bytes=64)
+            else:
+                grouped = ring.tile([P, P * PACK], BF16, name="wa_bf", tag="wa_bf", bufs=4, align_bytes=64)
+            nc.scalar.copy(
+                grouped[:].rearrange("p (u i j) -> p u j i", i=4, j=PACK),
+                wa_raw[b][:].rearrange("p j (u t i) -> p t u j i", t=PACK, i=4)[:, t],
+            )
+            return grouped
+
+        def quant_wa(j, grouped):
+            wa_codes[j] = keep.tile([P, P], U32, name="wa_codes%d" % j, align_bytes=64)
+            wa_scales[j] = keep.tile([P, P], U8, name="wa_scales%d" % j, align_bytes=64)
+            nc.vector.quantize_mx(out=wa_codes[j][:].bitcast(FP8X4), scales=wa_scales[j][:], in_=grouped[:])
+
+        h_tiles = {}
+
+        def stage1(j):
+            cols = slice(j * P, (j + 1) * P)
+            h_tiles[j] = ring.tile([P, S], F32, name="h", tag="h", bufs=3)
+            parts = []
+            for half in range(2):
+                tok = slice(half * BANK, (half + 1) * BANK)
+                rhs = vw[half][:].bitcast(FP8X4)
+                pb = psum.tile([P, BANK], F32, name="pb", tag="pb", bufs=2)
+                nc.tensor.matmul_mx(out=pb[:], lhsT=wb[:, j * 2 * P : (j + 1) * 2 * P].bitcast(FP4X4),
+                                    lhsT_scale=ws[:, cols], rhs=rhs, rhs_scale=vs[:, tok], start=True, stop=True)
+                pd = psum.tile([P, BANK], F32, name="pd", tag="pd", bufs=3)
+                nc.tensor.matmul_mx(out=pd[:], lhsT=wd[:, cols].bitcast(FP8X4),
+                                    lhsT_scale=ws[4:P, cols], rhs=rhs, rhs_scale=vs[:, tok], start=True, stop=True)
+                pa = psum.tile([P, BANK], F32, name="pa", tag="pa", bufs=3)
+                nc.tensor.matmul_mx(out=pa[:], lhsT=wa_codes[j][:].bitcast(FP8X4),
+                                    lhsT_scale=wa_scales[j][:], rhs=rhs, rhs_scale=vs[:, tok], start=True, stop=True)
+                b_sb = ring.tile([P, BANK], F32, name="b_sb", tag="b_sb", bufs=4)
+                nc.scalar.copy(b_sb[:], pb[:])
+                bd = ring.tile([P, BANK], F32, name="bd", tag="bd", bufs=3)
+                nc.vector.tensor_tensor(bd[:], pd[:], b_sb[:], ALU.mult)
+                parts.append((tok, pa, bd))
+            for tok, pa, bd in parts:
+                nc.vector.tensor_tensor(h_tiles[j][:, tok], pa[:], bd[:], ALU.add)
+
+        z32 = {}
+        for b in range(PASSES):
+            for half in range(2):
+                z32[b, half] = keep.tile([P, PACK, HALF], F32, name="z32_%d_%d" % (b, half))
+
+        def pick(j, halves):
+            b, t = divmod(j, PACK)
+            before = {}
+            for half in halves:
+                before[half] = ring.tile([P, HALF], F32, name="before", tag="before", bufs=4)
+                nc.vector.tensor_copy(before[half][:], h_tiles[j][:].indirect(pos2_sb[:, half * 16 : (half + 1) * 16]))
+            for half in halves:
+                nc.vector.tensor_tensor(z32[b, half][:, t, :], h_tiles[j][:].indirect(pos1_sb[:, half * 16 : (half + 1) * 16]),
+                                        before[half][:], ALU.subtract)
+
+        z_bf = {}
+        z_codes = {}
+        z_scales = {}
+
+        def cast_z(b, half, eng_copy):
+            z_bf[b, half] = keep.tile([P, HALF * PACK], BF16, name="z_bf%d_%d" % (b, half), align_bytes=64)
+            eng_copy(z_bf[b, half][:].rearrange("p (c i t) -> p c t i", i=4, t=PACK),
+                     z32[b, half][:].rearrange("p t (c i) -> p c t i", i=4))
+
+        def quant_z(b, half):
+            z_codes[b, half] = keep.tile([P, HALF], U32, name="z_codes%d_%d" % (b, half), align_bytes=64)
+            z_scales[b, half] = keep.tile([P, HALF], U8, name="z_scales%d_%d" % (b, half), align_bytes=64)
+            nc.vector.quantize_mx(out=z_codes[b, half][:].bitcast(FP8X4), scales=z_scales[b, half][:], in_=z_bf[b, half][:])
+
+        w2_bf = keep.tile([P, PASSES * N * PACK], BF16, name="w2_bf", align_bytes=64)
+        w2_codes = keep.tile([P, PASSES * N], U32, name="w2_codes", align_bytes=64)
+        w2_scales = keep.tile([P, PASSES * N], U8, name="w2_scales", align_bytes=64)
+
+        def cast_w2(piece):
+            b, c = divmod(piece, NT)
+            nc.scalar.copy(
+                w2_bf[:, piece * P * PACK : (piece + 1) * P * PACK].rearrange("p (c i t) -> p c t i", i=4, t=PACK),
+                w2_raw[b][:, :, c * P : (c + 1) * P].rearrange("p t (c i) -> p c t i", i=4),
+            )
+
+        def quant_w2(lo, hi):
+            nc.vector.quantize_mx(out=w2_codes[:, lo:hi].bitcast(FP8X4), scales=w2_scales[:, lo:hi],
+                                  in_=w2_bf[:, lo * PACK : hi * PACK])
+
+        out_rows = out.rearrange("(c p) m -> p c m", p=P)
+
+        def stage2(half):
+            res = keep.tile([P, NT, HALF], F32, name="res%d" % half)
+            for c, (tag, bufs) in enumerate((("pb", 2), ("pd", 3), ("pa", 3))):
+                py = psum.tile([P, HALF], F32, name="py", tag=tag, bufs=bufs)
+                for b in range(PASSES):
+                    cols = slice(b * N + c * P, b * N + (c + 1) * P)
+                    nc.tensor.matmul_mx(out=py[:], lhsT=w2_codes[:, cols].bitcast(FP8X4), lhsT_scale=w2_scales[:, cols],
+                                        rhs=z_codes[b, half][:].bitcast(FP8X4), rhs_scale=z_scales[b, half][:],
+                                        start=(b == 0), stop=(b == PASSES - 1))
+                nc.scalar.activation(res[:, c, :], py[:], ACT.Sigmoid, bias=neg_theta[:, c : c + 1])
+            nc.sync.dma_start(out_rows[:, :, half * HALF : (half + 1) * HALF], res[:])
+
+        tiles = PASSES * PACK
+        quant_wa(0, cast_wa(0))
+        w2_rows = w2.rearrange("(b u t i) n -> b t u i n", b=PASSES, t=PACK, i=4)
+        w2_raw = []
+        for b in range(PASSES):
+            w2_raw.append(keep.tile([P, PACK, N], F32, name="w2_raw", tag="raw%d" % b, align_bytes=64))
+            for t in range(PACK):
+                nc.sync.dma_start(w2_raw[b][:, t, :], w2_rows[b, t])
+
+        grouped = cast_wa(1)
+        for j in range(tiles):
+            stage1(j)
+            if j + 1 < tiles:
+                quant_wa(j + 1, grouped)
+            if j + 2 == PACK:
+                load_wa(1)
+            if j + 2 < tiles:
+                grouped = cast_wa(j + 2)
+            if 2 <= j < 2 + PASSES * NT // 2:
+                cast_w2(2 * (j - 2))
+                cast_w2(2 * (j - 2) + 1)
+            if 1 <= j < tiles - 1:
+                pick(j - 1, (0, 1))
+            if j == 4:
+                cast_z(0, 0, nc.scalar.copy)
+                cast_z(0, 1, nc.scalar.copy)
+            if j == 5:
+                quant_w2(0, 512)
+                quant_w2(512, 768)
+            if j == 6:
+                quant_z(0, 0)
+                quant_z(0, 1)
+        pick(6, (0,))
+        pick(7, (0,))
+        cast_z(1, 0, nc.scalar.copy)
+        pick(6, (1,))
+        pick(7, (1,))
+        quant_z(1, 0)
+        stage2(0)
+        cast_z(1, 1, nc.vector.tensor_copy)
+        quant_z(1, 1)
+        stage2(1)

@@ -19,9 +19,11 @@ ACT = mybir.ActivationFunctionType
 P = 128
 PACK = 4
 BANK = 512
-PASSES = H // (P * PACK)
+PASS = P * PACK
+PASSES = H // PASS
+TILES = PASSES * PACK
 NT = N // P
-HALF = NPAIR // 2
+PIECES = ((0, 256), (256, 384), (384, 512))
 
 
 def tile_list_sleep_arousal_scores_kernel(
@@ -37,211 +39,285 @@ def tile_list_sleep_arousal_scores_kernel(
         pos1_sb = keep.tile([P, NPAIR // 16], U16, name="pos1_sb")
         pos2_sb = keep.tile([P, NPAIR // 16], U16, name="pos2_sb")
 
+        def load_scale_rows(dst, src):
+            nc.sync.dma_start(dst.bitcast(I32), src[0].bitcast(I32).unsqueeze(1).broadcast_to([16, 8, src.shape[2] // 4]))
+
         tabs_sb = keep.tile([P, T], U8, name="tabs_sb", align_bytes=64)
         tabw_sb = keep.tile([P, T], I32, name="tabw_sb", align_bytes=64)
-        ws_raw = keep.tile([P, H], U8, name="ws_raw", tag="raw0", align_bytes=64)
-        vs = keep.tile([P, S], U8, name="vs", align_bytes=64)
-        wb_raw = keep.tile([P, 2 * H], U8, name="wb_raw", align_bytes=64)
-        wd_raw = keep.tile([P, H], I32, name="wd_raw", align_bytes=64)
+        wbs_raw = keep.tile([P, H], U8, name="wbs_raw", align_bytes=64)
+        wds_raw = keep.tile([P, H], U8, name="wds_raw", align_bytes=64)
+        planes = keep.tile([P, S + 2 * H], U8, name="planes", align_bytes=64)
+        nc.vector.memset(planes[:].bitcast(I32), 0)
 
-        nc.vector.memset(vs[:].bitcast(I32), 0)
-
-        nc.sync.dma_start(tabs_sb[:].bitcast(I32), tab_scales[0].bitcast(I32).unsqueeze(1).broadcast_to([16, 8, T // 4]))
+        load_scale_rows(tabs_sb[:], tab_scales)
         nc.sync.dma_start(offs_sb[:], offs)
+        load_scale_rows(wbs_raw[:], wb_scales)
+        load_scale_rows(wds_raw[:], wd_scales)
         nc.sync.dma_start(tabw_sb[:], tab_words[0].rearrange("p t i -> p (t i)").bitcast(I32))
-        for r in range(4):
-            nc.scalar.dma_start(ws_raw[r:P:8, :].bitcast(I32), wb_scales[0, r:16:4, :].bitcast(I32).unsqueeze(1).broadcast_to([4, 4, H // 4]))
-        nc.sync.dma_start(wb_raw[:].bitcast(I32), wb_words[0].bitcast(I32))
-        nc.sync.dma_start(wd_raw[:], wd_words[0].rearrange("p c i -> p (c i)").bitcast(I32))
-        for r in range(4):
-            nc.gpsimd.dma_start(ws_raw[4 + r : P : 8, :].bitcast(I32), wd_scales[0, r:16:4, :].bitcast(I32).unsqueeze(1).broadcast_to([4, 4, H // 4]))
+
+        wb_rows = wb_words[0].bitcast(I32)
+        wd_rows = wd_words[0].rearrange("p c i -> p (c i)").bitcast(I32)
         wa_rows = wa.rearrange("(p j) c -> p j c", j=PACK)
-        wa_raw = {}
+        wb_raw, wd_raw, wa_raw, wb, wd = {}, {}, {}, {}, {}
+
+        def load_packed(b):
+            wb_raw[b] = keep.tile([P, PASS // 2], I32, name="wb_raw", tag="wb_raw")
+            nc.sync.dma_start(wb_raw[b][:], wb_rows[:, b * PASS // 2 : (b + 1) * PASS // 2])
+            wd_raw[b] = keep.tile([P, PASS], I32, name="wd_raw", tag="wd_raw")
+            nc.sync.dma_start(wd_raw[b][:], wd_rows[:, b * PASS : (b + 1) * PASS])
 
         def load_wa(b):
-            wa_raw[b] = keep.tile([P, PACK, 512], F32, name="wa_raw", tag="wa_raw")
-            nc.sync.dma_start(wa_raw[b][:], wa_rows[:, :, b * 512 : (b + 1) * 512])
+            wa_raw[b] = keep.tile([P, PACK, PASS], F32, name="wa_raw", tag="wa_raw")
+            nc.sync.dma_start(wa_raw[b][:], wa_rows[:, :, b * PASS : (b + 1) * PASS])
 
+        def deal_packed(b):
+            wb[b] = keep.tile([P, 2 * PASS], U8, name="wb%d" % b, align_bytes=64)
+            nc.vector.tensor_copy(
+                wb[b][:].bitcast(I32).rearrange("p (t u i) -> p u t i", t=PACK, i=2),
+                wb_raw[b][:].rearrange("p (u t i) -> p u t i", t=PACK, i=2),
+            )
+            wd[b] = keep.tile([P, PASS], I32, name="wd%d" % b, align_bytes=64)
+            nc.vector.tensor_copy(
+                wd[b][:].rearrange("p (t u i) -> p u t i", t=PACK, i=4),
+                wd_raw[b][:].rearrange("p (u t i) -> p u t i", t=PACK, i=4),
+            )
+
+        load_packed(0)
         load_wa(0)
         nc.sync.dma_start(pos1_sb[:], pos1)
         nc.sync.dma_start(pos2_sb[:], pos2)
-
-        vs_picked = keep.tile([P, S], U8, name="vs_picked", align_bytes=64)
-        nc.vector.tensor_copy(vs_picked[:], tabs_sb[:].indirect(offs_sb[:]))
-        for r in range(4):
-            nc.scalar.dma_start(vs[32 * r : 32 * r + 4, :].bitcast(I32), vs_picked[32 * r : 32 * r + 32 : 8, :].bitcast(I32))
-        vw = []
-        for half in range(2):
-            vw.append(keep.tile([P, BANK], U32, name="vw%d" % half, align_bytes=64))
-            nc.vector.tensor_copy(
-                vw[half][:], tabw_sb[:].bitcast(U32).indirect(offs_sb[:, half * 32 : (half + 1) * 32])
-            )
-
         theta_sb = keep.tile([P, NT], F32, name="theta_sb")
         with nc.allow_non_contiguous_dma(reason="one threshold a partition"):
             nc.gpsimd.dma_start(theta_sb[:], theta.rearrange("(c p) -> p c", p=P))
         neg_theta = keep.tile([P, NT], F32, name="neg_theta")
         nc.gpsimd.tensor_scalar(neg_theta[:], theta_sb[:], -1.0, 0.0, ALU.mult, ALU.add)
 
-        ws = keep.tile([P, H], U8, name="ws", align_bytes=64)
-        nc.vector.tensor_copy(
-            ws[:].bitcast(I32).rearrange("p (b t u) -> p b t u", b=PASSES, t=PACK),
-            ws_raw[:].bitcast(I32).rearrange("p (b u t) -> p b t u", b=PASSES, t=PACK),
-        )
-        wb = keep.tile([P, 2 * H], U8, name="wb", align_bytes=64)
-        nc.vector.tensor_copy(
-            wb[:].bitcast(I32).rearrange("p (b t u i) -> p b u t i", b=PASSES, t=PACK, i=2),
-            wb_raw[:].bitcast(I32).rearrange("p (b u t i) -> p b u t i", b=PASSES, t=PACK, i=2),
-        )
-        wd = keep.tile([P, H], I32, name="wd", align_bytes=64)
-        nc.vector.tensor_copy(
-            wd[:].rearrange("p (b t u i) -> p b u t i", b=PASSES, t=PACK, i=4),
-            wd_raw[:].rearrange("p (b u t i) -> p b u t i", b=PASSES, t=PACK, i=4),
-        )
+        vs_picked = keep.tile([P, S], U8, name="vs_picked", align_bytes=64)
+        nc.vector.tensor_copy(vs_picked[:], tabs_sb[:].indirect(offs_sb[:]))
+        staged = keep.tile([P, (S + 2 * H) // 4], I32, name="staged", tag="early0", align_bytes=64)
+        for at, raw in ((S // 4, wbs_raw), ((S + H) // 4, wds_raw)):
+            nc.vector.tensor_copy(
+                staged[:, at : at + H // 4].rearrange("p (b t u) -> p b t u", b=PASSES, t=PACK),
+                raw[:].bitcast(I32).rearrange("p (b u t) -> p b t u", b=PASSES, t=PACK),
+            )
+        nc.vector.tensor_copy(staged[:, 0 : S // 4], vs_picked[:].bitcast(I32))
+        for q in range(4):
+            nc.scalar.dma_start(planes[32 * q : 32 * q + 4, :].bitcast(I32), staged[32 * q : 32 * q + 32 : 8, :])
 
-        wa_codes = {}
-        wa_scales = {}
+        vw = []
+
+        def pick_words(half):
+            vw.append(keep.tile([P, BANK], U32, name="vw%d" % half, align_bytes=64))
+            nc.vector.tensor_copy(
+                vw[half][:], tabw_sb[:].bitcast(U32).indirect(offs_sb[:, half * 32 : (half + 1) * 32])
+            )
+
+        wa_groups = ((0, 1), (1, 2), (2, 4), (4, 8))
+        wa_bf, wa_codes, wa_scales = {}, {}, {}
 
         def cast_wa(j):
             b, t = divmod(j, PACK)
-            if j == 0:
-                grouped = keep.tile([P, P * PACK], BF16, name="wa_bf0", tag="raw1", align_bytes=64)
-            else:
-                grouped = ring.tile([P, P * PACK], BF16, name="wa_bf", tag="wa_bf", bufs=4, align_bytes=64)
+            lo, hi = [g for g in wa_groups if g[0] <= j < g[1]][0]
+            if j == lo:
+                wa_bf[lo] = keep.tile([P, (hi - lo) * PASS], BF16, name="wa_bf%d" % lo,
+                                      tag="early1" if j == 0 else "wa_bf%d" % lo, align_bytes=64)
             nc.scalar.copy(
-                grouped[:].rearrange("p (u i j) -> p u j i", i=4, j=PACK),
+                wa_bf[lo][:, (j - lo) * PASS : (j - lo + 1) * PASS].rearrange("p (u i j) -> p u j i", i=4, j=PACK),
                 wa_raw[b][:].rearrange("p j (u t i) -> p t u j i", t=PACK, i=4)[:, t],
             )
-            return grouped
 
-        def quant_wa(j, grouped):
-            wa_codes[j] = keep.tile([P, P], U32, name="wa_codes%d" % j, align_bytes=64)
-            wa_scales[j] = keep.tile([P, P], U8, name="wa_scales%d" % j, align_bytes=64)
-            nc.vector.quantize_mx(out=wa_codes[j][:].bitcast(FP8X4), scales=wa_scales[j][:], in_=grouped[:])
+        def quant_wa(lo, hi):
+            codes = keep.tile([P, (hi - lo) * P], U32, name="wa_codes%d" % lo, tag="wa_codes%d" % lo, align_bytes=64)
+            scales = keep.tile([P, (hi - lo) * P], U8, name="wa_scales%d" % lo, align_bytes=64)
+            nc.vector.quantize_mx(out=codes[:].bitcast(FP8X4), scales=scales[:], in_=wa_bf[lo][:])
+            for j in range(lo, hi):
+                wa_codes[j] = codes[:, (j - lo) * P : (j - lo + 1) * P]
+                wa_scales[j] = scales[:, (j - lo) * P : (j - lo + 1) * P]
 
-        h_tiles = {}
+        held = {5: "w2_codes", 7: "z_codes0_0"}
+        b_tiles, bd_tiles, a_tiles, h_tiles = {}, {}, {}, {}
 
-        def stage1(j):
-            cols = slice(j * P, (j + 1) * P)
-            h_tiles[j] = ring.tile([P, S], F32, name="h", tag="h", bufs=3)
-            parts = []
-            for half in range(2):
-                tok = slice(half * BANK, (half + 1) * BANK)
-                rhs = vw[half][:].bitcast(FP8X4)
-                pb = psum.tile([P, BANK], F32, name="pb", tag="pb", bufs=2)
-                nc.tensor.matmul_mx(out=pb[:], lhsT=wb[:, j * 2 * P : (j + 1) * 2 * P].bitcast(FP4X4),
-                                    lhsT_scale=ws[:, cols], rhs=rhs, rhs_scale=vs[:, tok], start=True, stop=True)
-                pd = psum.tile([P, BANK], F32, name="pd", tag="pd", bufs=3)
-                nc.tensor.matmul_mx(out=pd[:], lhsT=wd[:, cols].bitcast(FP8X4),
-                                    lhsT_scale=ws[4:P, cols], rhs=rhs, rhs_scale=vs[:, tok], start=True, stop=True)
-                pa = psum.tile([P, BANK], F32, name="pa", tag="pa", bufs=3)
-                nc.tensor.matmul_mx(out=pa[:], lhsT=wa_codes[j][:].bitcast(FP8X4),
-                                    lhsT_scale=wa_scales[j][:], rhs=rhs, rhs_scale=vs[:, tok], start=True, stop=True)
-                b_sb = ring.tile([P, BANK], F32, name="b_sb", tag="b_sb", bufs=4)
-                nc.scalar.copy(b_sb[:], pb[:])
-                bd = ring.tile([P, BANK], F32, name="bd", tag="bd", bufs=3)
-                nc.vector.tensor_tensor(bd[:], pd[:], b_sb[:], ALU.mult)
-                parts.append((tok, pa, bd))
-            for tok, pa, bd in parts:
-                nc.vector.tensor_tensor(h_tiles[j][:, tok], pa[:], bd[:], ALU.add)
-
-        z32 = {}
-        for b in range(PASSES):
-            for half in range(2):
-                z32[b, half] = keep.tile([P, PACK, HALF], F32, name="z32_%d_%d" % (b, half))
-
-        def pick(j, halves):
+        def products(j, *halves):
             b, t = divmod(j, PACK)
-            before = {}
             for half in halves:
-                before[half] = ring.tile([P, HALF], F32, name="before", tag="before", bufs=4)
-                nc.vector.tensor_copy(before[half][:], h_tiles[j][:].indirect(pos2_sb[:, half * 16 : (half + 1) * 16]))
-            for half in halves:
-                nc.vector.tensor_tensor(z32[b, half][:, t, :], h_tiles[j][:].indirect(pos1_sb[:, half * 16 : (half + 1) * 16]),
-                                        before[half][:], ALU.subtract)
+                rhs = vw[half][:].bitcast(FP8X4)
+                rhs_scale = planes[:, half * BANK : (half + 1) * BANK]
+                pb = psum.tile([P, BANK], F32, name="pb", tag="pb", bufs=2)
+                nc.tensor.matmul_mx(out=pb[:], lhsT=wb[b][:, t * 2 * P : (t + 1) * 2 * P].bitcast(FP4X4),
+                                    lhsT_scale=planes[:, S + j * P : S + (j + 1) * P],
+                                    rhs=rhs, rhs_scale=rhs_scale, start=True, stop=True)
+                pd = psum.tile([P, BANK], F32, name="pd", tag="pd", bufs=3)
+                nc.tensor.matmul_mx(out=pd[:], lhsT=wd[b][:, t * P : (t + 1) * P].bitcast(FP8X4),
+                                    lhsT_scale=planes[:, S + H + j * P : S + H + (j + 1) * P],
+                                    rhs=rhs, rhs_scale=rhs_scale, start=True, stop=True)
+                if half == 0:
+                    b_sb = ring.tile([P, BANK], F32, name="b0", tag="b0", bufs=2)
+                elif j in held:
+                    b_sb = keep.tile([P, BANK], F32, name="b_held", tag=held[j], align_bytes=64)
+                else:
+                    b_sb = ring.tile([P, BANK], F32, name="b1", tag="b1", bufs=6)
+                b_tiles[j, half] = b_sb
+                nc.scalar.copy(b_sb[:], pb[:])
+                if (j, half) == (2, 1):
+                    bd = keep.tile([P, BANK], F32, name="bd_held", tag="wa_codes4", align_bytes=64)
+                elif j < 3 or (j, half) == (4, 0):
+                    bd = ring.tile([P, BANK], F32, name="bd", tag="bd", bufs=5)
+                elif half == 0:
+                    bd = bd_tiles[j - 2, 1]
+                else:
+                    bd = b_tiles[j - 1, 1]
+                bd_tiles[j, half] = bd
+                nc.vector.tensor_tensor(bd[:], pd[:], b_sb[:], ALU.mult)
 
-        z_bf = {}
-        z_codes = {}
-        z_scales = {}
+        def linear(j, half):
+            pa = psum.tile([P, BANK], F32, name="pa", tag="pa", bufs=3)
+            nc.tensor.matmul_mx(out=pa[:], lhsT=wa_codes[j].bitcast(FP8X4), lhsT_scale=wa_scales[j],
+                                rhs=vw[half][:].bitcast(FP8X4), rhs_scale=planes[:, half * BANK : (half + 1) * BANK],
+                                start=True, stop=True)
+            return pa
 
-        def cast_z(b, half, eng_copy):
-            z_bf[b, half] = keep.tile([P, HALF * PACK], BF16, name="z_bf%d_%d" % (b, half), align_bytes=64)
-            eng_copy(z_bf[b, half][:].rearrange("p (c i t) -> p c t i", i=4, t=PACK),
-                     z32[b, half][:].rearrange("p t (c i) -> p c t i", i=4))
+        def linear_first(j):
+            a_tiles[j] = ring.tile([P, BANK], F32, name="a_sb", tag="a_sb", bufs=2)
+            nc.scalar.copy(a_tiles[j][:], linear(j, 0)[:])
 
-        def quant_z(b, half):
-            z_codes[b, half] = keep.tile([P, HALF], U32, name="z_codes%d_%d" % (b, half), align_bytes=64)
-            z_scales[b, half] = keep.tile([P, HALF], U8, name="z_scales%d_%d" % (b, half), align_bytes=64)
-            nc.vector.quantize_mx(out=z_codes[b, half][:].bitcast(FP8X4), scales=z_scales[b, half][:], in_=z_bf[b, half][:])
+        def join(j):
+            h_tiles[j] = ring.tile([P, S], F32, name="h", tag="h", bufs=2)
+            if j + 1 < TILES:
+                nc.gpsimd.tensor_tensor(h_tiles[j][:, 0:BANK], a_tiles[j][:], bd_tiles[j, 0][:], ALU.add)
+            else:
+                nc.vector.tensor_tensor(h_tiles[j][:, 0:BANK], linear(j, 0)[:], bd_tiles[j, 0][:], ALU.add)
+            nc.vector.tensor_tensor(h_tiles[j][:, BANK:S], linear(j, 1)[:], bd_tiles[j, 1][:], ALU.add)
+
+        z32 = [keep.tile([P, PACK, NPAIR], F32, name="z32_%d" % b) for b in range(PASSES)]
+
+        def pick(j, lo, hi, before):
+            b, t = divmod(j, PACK)
+            nc.vector.tensor_copy(before, h_tiles[j][:].indirect(pos2_sb[:, lo // 16 : hi // 16]))
+            return lambda: nc.vector.tensor_tensor(
+                z32[b][:, t, lo:hi], h_tiles[j][:].indirect(pos1_sb[:, lo // 16 : hi // 16]), before, ALU.subtract)
+
+        z_bf = [keep.tile([P, NPAIR * PACK], BF16, name="z_bf%d" % b, align_bytes=64) for b in range(PASSES)]
+        z_codes, z_scales = {}, {}
+
+        def cast_z(b, lo, hi, copy):
+            copy(z_bf[b][:, lo * PACK : hi * PACK].rearrange("p (c i t) -> p c t i", i=4, t=PACK),
+                 z32[b][:, :, lo:hi].rearrange("p t (c i) -> p c t i", i=4))
+
+        def quant_z(b, lo, hi):
+            z_codes[b, lo] = keep.tile([P, hi - lo], U32, name="z_codes%d_%d" % (b, lo), tag="z_codes%d_%d" % (b, lo), align_bytes=64)
+            z_scales[b, lo] = keep.tile([P, hi - lo], U8, name="z_scales%d_%d" % (b, lo), align_bytes=64)
+            nc.vector.quantize_mx(out=z_codes[b, lo][:].bitcast(FP8X4), scales=z_scales[b, lo][:],
+                                  in_=z_bf[b][:, lo * PACK : hi * PACK])
+
+        w2_rows = w2.rearrange("(b u t i) n -> b t u i n", b=PASSES, t=PACK, i=4)
+        w2_raw = {}
+
+        def load_w2(b):
+            w2_raw[b] = keep.tile([P, PACK, N], F32, name="w2_raw", tag="early%d" % b, align_bytes=64)
+            for t in range(PACK):
+                nc.sync.dma_start(w2_raw[b][:, t, :], w2_rows[b, t])
 
         w2_bf = keep.tile([P, PASSES * N * PACK], BF16, name="w2_bf", align_bytes=64)
-        w2_codes = keep.tile([P, PASSES * N], U32, name="w2_codes", align_bytes=64)
+        w2_codes = []
         w2_scales = keep.tile([P, PASSES * N], U8, name="w2_scales", align_bytes=64)
 
         def cast_w2(piece):
             b, c = divmod(piece, NT)
             nc.scalar.copy(
-                w2_bf[:, piece * P * PACK : (piece + 1) * P * PACK].rearrange("p (c i t) -> p c t i", i=4, t=PACK),
+                w2_bf[:, piece * PASS : (piece + 1) * PASS].rearrange("p (c i t) -> p c t i", i=4, t=PACK),
                 w2_raw[b][:, :, c * P : (c + 1) * P].rearrange("p t (c i) -> p c t i", i=4),
             )
 
-        def quant_w2(lo, hi):
-            nc.vector.quantize_mx(out=w2_codes[:, lo:hi].bitcast(FP8X4), scales=w2_scales[:, lo:hi],
-                                  in_=w2_bf[:, lo * PACK : hi * PACK])
+        def quant_w2():
+            w2_codes.append(keep.tile([P, PASSES * N], U32, name="w2_codes", tag="w2_codes", align_bytes=64))
+            for lo, hi in ((0, 512), (512, PASSES * N)):
+                nc.vector.quantize_mx(out=w2_codes[0][:, lo:hi].bitcast(FP8X4), scales=w2_scales[:, lo:hi],
+                                      in_=w2_bf[:, lo * PACK : hi * PACK])
 
         out_rows = out.rearrange("(c p) m -> p c m", p=P)
+        bank_tags = (("pb", 2), ("pd", 3), ("pa", 3))
+        y_banks = {}
 
-        def stage2(half):
-            res = keep.tile([P, NT, HALF], F32, name="res%d" % half)
-            for c, (tag, bufs) in enumerate((("pb", 2), ("pd", 3), ("pa", 3))):
-                py = psum.tile([P, HALF], F32, name="py", tag=tag, bufs=bufs)
-                for b in range(PASSES):
-                    cols = slice(b * N + c * P, b * N + (c + 1) * P)
-                    nc.tensor.matmul_mx(out=py[:], lhsT=w2_codes[:, cols].bitcast(FP8X4), lhsT_scale=w2_scales[:, cols],
-                                        rhs=z_codes[b, half][:].bitcast(FP8X4), rhs_scale=z_scales[b, half][:],
-                                        start=(b == 0), stop=(b == PASSES - 1))
-                nc.scalar.activation(res[:, c, :], py[:], ACT.Sigmoid, bias=neg_theta[:, c : c + 1])
-            nc.sync.dma_start(out_rows[:, :, half * HALF : (half + 1) * HALF], res[:])
+        def scores_pass(b, lo, hi):
+            for c in range(NT):
+                if b == 0:
+                    y_banks[lo, c] = psum.tile([P, hi - lo], F32, name="py", tag=bank_tags[c][0], bufs=bank_tags[c][1])
+                    rhs, rhs_scale = z_codes[0, 0][:, lo:hi], z_scales[0, 0][:, lo:hi]
+                else:
+                    rhs, rhs_scale = z_codes[b, lo][:], z_scales[b, lo][:]
+                cols = slice(b * N + c * P, b * N + (c + 1) * P)
+                nc.tensor.matmul_mx(out=y_banks[lo, c][:], lhsT=w2_codes[0][:, cols].bitcast(FP8X4),
+                                    lhsT_scale=w2_scales[:, cols], rhs=rhs.bitcast(FP8X4), rhs_scale=rhs_scale,
+                                    start=(b == 0), stop=(b == PASSES - 1))
 
-        tiles = PASSES * PACK
-        quant_wa(0, cast_wa(0))
-        w2_rows = w2.rearrange("(b u t i) n -> b t u i n", b=PASSES, t=PACK, i=4)
-        w2_raw = []
-        for b in range(PASSES):
-            w2_raw.append(keep.tile([P, PACK, N], F32, name="w2_raw", tag="raw%d" % b, align_bytes=64))
-            for t in range(PACK):
-                nc.sync.dma_start(w2_raw[b][:, t, :], w2_rows[b, t])
+        def finish(lo, hi):
+            res = keep.tile([P, NT, hi - lo], F32, name="res%d" % lo)
+            for c in range(NT):
+                nc.scalar.activation(res[:, c, :], y_banks[lo, c][:], ACT.Sigmoid, bias=neg_theta[:, c : c + 1])
+            nc.sync.dma_start(out_rows[:, :, lo:hi], res[:])
 
-        grouped = cast_wa(1)
-        for j in range(tiles):
-            stage1(j)
-            if j + 1 < tiles:
-                quant_wa(j + 1, grouped)
-            if j + 2 == PACK:
-                load_wa(1)
-            if j + 2 < tiles:
-                grouped = cast_wa(j + 2)
-            if 2 <= j < 2 + PASSES * NT // 2:
-                cast_w2(2 * (j - 2))
-                cast_w2(2 * (j - 2) + 1)
-            if 1 <= j < tiles - 1:
-                pick(j - 1, (0, 1))
+        pick_words(0)
+        deal_packed(0)
+        pick_words(1)
+        load_packed(1)
+        cast_wa(0)
+        products(0, 0, 1)
+        quant_wa(0, 1)
+        load_w2(0)
+        load_w2(1)
+        cast_wa(1)
+        linear_first(0)
+        join(0)
+        products(1, 0, 1)
+        quant_wa(1, 2)
+        deal_packed(1)
+        cast_wa(2)
+        cast_wa(3)
+        load_wa(1)
+        linear_first(1)
+        quant_wa(2, 4)
+        for j in range(TILES - 2):
+            products(j + 2, 0)
+            join(j + 1)
+            products(j + 2, 1)
+            if j < 2:
+                cast_wa(4 + 2 * j)
+                cast_wa(5 + 2 * j)
+            if j + 3 < TILES:
+                linear_first(j + 2)
+            if 1 <= j < 1 + NT:
+                cast_w2(2 * (j - 1))
+                cast_w2(2 * (j - 1) + 1)
+            first_sub = pick(j, 0, 256, bd_tiles[j + 1, 1][:, 0:256])
+            second_sub = pick(j, 256, 512, b_tiles[j + 2, 1][:, 0:256])
+            first_sub()
+            second_sub()
+            if j == 1:
+                quant_wa(4, 8)
+            if j == 3:
+                cast_z(0, 0, 256, nc.scalar.copy)
             if j == 4:
-                cast_z(0, 0, nc.scalar.copy)
-                cast_z(0, 1, nc.scalar.copy)
+                cast_z(0, 256, 512, nc.scalar.copy)
             if j == 5:
-                quant_w2(0, 512)
-                quant_w2(512, 768)
-            if j == 6:
-                quant_z(0, 0)
-                quant_z(0, 1)
-        pick(6, (0,))
-        pick(7, (0,))
-        cast_z(1, 0, nc.scalar.copy)
-        pick(6, (1,))
-        pick(7, (1,))
-        quant_z(1, 0)
-        stage2(0)
-        cast_z(1, 1, nc.vector.tensor_copy)
-        quant_z(1, 1)
-        stage2(1)
+                quant_w2()
+                quant_z(0, 0, NPAIR)
+        join(TILES - 1)
+        scores_pass(0, *PIECES[0])
+        scores_pass(0, *PIECES[1])
+        for n, (lo, hi) in enumerate(PIECES):
+            last = n == len(PIECES) - 1
+            before = ring.tile([P, 2, hi - lo], F32, name="before", tag="before", bufs=2)
+            first_sub = pick(TILES - 2, lo, hi, before[:, 0, :])
+            second_sub = pick(TILES - 1, lo, hi, before[:, 1, :])
+            first_sub()
+            second_sub()
+            if n > 0:
+                quant_z(1, *PIECES[n - 1])
+                scores_pass(1, *PIECES[n - 1])
+                finish(*PIECES[n - 1])
+            if n == 1:
+                scores_pass(0, *PIECES[2])
+            cast_z(1, lo, hi, nc.vector.tensor_copy if last else nc.scalar.copy)
+        quant_z(1, lo, hi)
+        scores_pass(1, lo, hi)
+        finish(lo, hi)

@@ -67,7 +67,7 @@ def tile_list_sleep_arousal_scores_kernel(
             nc.sync.dma_start(wd_raw[b][:], wd_rows[:, b * PASS : (b + 1) * PASS])
 
         def load_wa(b):
-            wa_raw[b] = keep.tile([P, PACK, PASS], F32, name="wa_raw", tag="wa_raw")
+            wa_raw[b] = keep.tile([P, PACK, PASS], F32, name="wa_raw", tag=("wa_raw", "early0")[b], align_bytes=64)
             nc.sync.dma_start(wa_raw[b][:], wa_rows[:, :, b * PASS : (b + 1) * PASS])
 
         def deal_packed(b):
@@ -112,16 +112,16 @@ def tile_list_sleep_arousal_scores_kernel(
                 vw[half][:], tabw_sb[:].bitcast(U32).indirect(offs_sb[:, half * 32 : (half + 1) * 32])
             )
 
-        wa_groups = ((0, 1), (1, 2), (2, 4), (4, 8))
+        wa_groups = ((0, 2), (2, 4), (4, 8))
         wa_bf, wa_codes, wa_scales = {}, {}, {}
 
-        def cast_wa(j):
+        def cast_wa(j, copy):
             b, t = divmod(j, PACK)
             lo, hi = [g for g in wa_groups if g[0] <= j < g[1]][0]
             if j == lo:
                 wa_bf[lo] = keep.tile([P, (hi - lo) * PASS], BF16, name="wa_bf%d" % lo,
                                       tag="early1" if j == 0 else "wa_bf%d" % lo, align_bytes=64)
-            nc.scalar.copy(
+            copy(
                 wa_bf[lo][:, (j - lo) * PASS : (j - lo + 1) * PASS].rearrange("p (u i j) -> p u j i", i=4, j=PACK),
                 wa_raw[b][:].rearrange("p j (u t i) -> p t u j i", t=PACK, i=4)[:, t],
             )
@@ -134,7 +134,7 @@ def tile_list_sleep_arousal_scores_kernel(
                 wa_codes[j] = codes[:, (j - lo) * P : (j - lo + 1) * P]
                 wa_scales[j] = scales[:, (j - lo) * P : (j - lo + 1) * P]
 
-        held = {5: "w2_codes", 7: "z_codes0_0"}
+        held = {(3, 0): "wa_codes4", (7, 0): "w2_codes", (7, 1): "z_codes0_0"}
         b_tiles, bd_tiles, a_tiles, h_tiles = {}, {}, {}, {}
 
         def products(j, *halves):
@@ -150,22 +150,16 @@ def tile_list_sleep_arousal_scores_kernel(
                 nc.tensor.matmul_mx(out=pd[:], lhsT=wd[b][:, t * P : (t + 1) * P].bitcast(FP8X4),
                                     lhsT_scale=planes[:, S + H + j * P : S + H + (j + 1) * P],
                                     rhs=rhs, rhs_scale=rhs_scale, start=True, stop=True)
-                if half == 0:
-                    b_sb = ring.tile([P, BANK], F32, name="b0", tag="b0", bufs=2)
-                elif j in held:
-                    b_sb = keep.tile([P, BANK], F32, name="b_held", tag=held[j], align_bytes=64)
+                if (j, half) in held:
+                    b_sb = keep.tile([P, BANK], F32, name="b_held", tag=held[j, half], align_bytes=64)
                 else:
-                    b_sb = ring.tile([P, BANK], F32, name="b1", tag="b1", bufs=6)
+                    b_sb = ring.tile([P, BANK], F32, name="b_sb", tag="b_sb", bufs=8)
                 b_tiles[j, half] = b_sb
                 nc.scalar.copy(b_sb[:], pb[:])
-                if (j, half) == (2, 1):
-                    bd = keep.tile([P, BANK], F32, name="bd_held", tag="wa_codes4", align_bytes=64)
-                elif j < 3 or (j, half) == (4, 0):
-                    bd = ring.tile([P, BANK], F32, name="bd", tag="bd", bufs=5)
-                elif half == 0:
-                    bd = bd_tiles[j - 2, 1]
+                if j < 3 or (j, half) == (4, 0):
+                    bd = ring.tile([P, BANK], F32, name="bd", tag="bd", bufs=6)
                 else:
-                    bd = b_tiles[j - 1, 1]
+                    bd = b_tiles[j - 1, half]
                 bd_tiles[j, half] = bd
                 nc.vector.tensor_tensor(bd[:], pd[:], b_sb[:], ALU.mult)
 
@@ -177,16 +171,18 @@ def tile_list_sleep_arousal_scores_kernel(
             return pa
 
         def linear_first(j):
-            a_tiles[j] = ring.tile([P, BANK], F32, name="a_sb", tag="a_sb", bufs=2)
-            nc.scalar.copy(a_tiles[j][:], linear(j, 0)[:])
+            for half in range(2):
+                a_tiles[j, half] = ring.tile([P, BANK], F32, name="a_sb", tag="a_sb", bufs=4)
+                nc.scalar.copy(a_tiles[j, half][:], linear(j, half)[:])
 
         def join(j):
             h_tiles[j] = ring.tile([P, S], F32, name="h", tag="h", bufs=2)
-            if j + 1 < TILES:
-                nc.gpsimd.tensor_tensor(h_tiles[j][:, 0:BANK], a_tiles[j][:], bd_tiles[j, 0][:], ALU.add)
-            else:
-                nc.vector.tensor_tensor(h_tiles[j][:, 0:BANK], linear(j, 0)[:], bd_tiles[j, 0][:], ALU.add)
-            nc.vector.tensor_tensor(h_tiles[j][:, BANK:S], linear(j, 1)[:], bd_tiles[j, 1][:], ALU.add)
+            for half in range(2):
+                cols = slice(half * BANK, (half + 1) * BANK)
+                if 0 < j < TILES - 1:
+                    nc.gpsimd.tensor_tensor(h_tiles[j][:, cols], a_tiles[j, half][:], bd_tiles[j, half][:], ALU.add)
+                else:
+                    nc.vector.tensor_tensor(h_tiles[j][:, cols], linear(j, half)[:], bd_tiles[j, half][:], ALU.add)
 
         z32 = [keep.tile([P, PACK, NPAIR], F32, name="z32_%d" % b) for b in range(PASSES)]
 
@@ -213,7 +209,7 @@ def tile_list_sleep_arousal_scores_kernel(
         w2_raw = {}
 
         def load_w2(b):
-            w2_raw[b] = keep.tile([P, PACK, N], F32, name="w2_raw", tag="early%d" % b, align_bytes=64)
+            w2_raw[b] = keep.tile([P, PACK, N], F32, name="w2_raw", tag=("early1", "wa_raw")[b], align_bytes=64)
             for t in range(PACK):
                 nc.sync.dma_start(w2_raw[b][:, t, :], w2_rows[b, t])
 
@@ -260,48 +256,48 @@ def tile_list_sleep_arousal_scores_kernel(
         deal_packed(0)
         pick_words(1)
         load_packed(1)
-        cast_wa(0)
-        products(0, 0, 1)
-        quant_wa(0, 1)
-        load_w2(0)
-        load_w2(1)
-        cast_wa(1)
-        linear_first(0)
-        join(0)
-        products(1, 0, 1)
-        quant_wa(1, 2)
-        deal_packed(1)
-        cast_wa(2)
-        cast_wa(3)
         load_wa(1)
+        cast_wa(0, nc.vector.tensor_copy)
+        cast_wa(1, nc.vector.tensor_copy)
+        products(0, 0)
+        quant_wa(0, 2)
+        load_w2(0)
+        products(0, 1)
+        products(1, 0)
+        join(0)
+        products(1, 1)
         linear_first(1)
-        quant_wa(2, 4)
+        deal_packed(1)
         for j in range(TILES - 2):
             products(j + 2, 0)
             join(j + 1)
             products(j + 2, 1)
-            if j < 2:
-                cast_wa(4 + 2 * j)
-                cast_wa(5 + 2 * j)
+            if j == 0:
+                cast_wa(2, nc.scalar.copy)
+                cast_wa(3, nc.scalar.copy)
+                quant_wa(2, 4)
+                load_w2(1)
+            if j == 1:
+                for t in range(PACK):
+                    cast_wa(PACK + t, nc.scalar.copy)
             if j + 3 < TILES:
                 linear_first(j + 2)
-            if 1 <= j < 1 + NT:
-                cast_w2(2 * (j - 1))
-                cast_w2(2 * (j - 1) + 1)
-            first_sub = pick(j, 0, 256, bd_tiles[j + 1, 1][:, 0:256])
+            if 2 <= j < 5:
+                cast_w2(j - 2)
+            if j == 5:
+                for piece in range(NT, 2 * NT):
+                    cast_w2(piece)
+                cast_z(0, 0, 256, nc.scalar.copy)
+                cast_z(0, 256, 512, nc.scalar.copy)
+            first_sub = pick(j, 0, 256, b_tiles[j + 2, 0][:, 0:256])
             second_sub = pick(j, 256, 512, b_tiles[j + 2, 1][:, 0:256])
             first_sub()
             second_sub()
             if j == 1:
                 quant_wa(4, 8)
-            if j == 3:
-                cast_z(0, 0, 256, nc.scalar.copy)
-            if j == 4:
-                cast_z(0, 256, 512, nc.scalar.copy)
-            if j == 5:
-                quant_w2()
-                quant_z(0, 0, NPAIR)
         join(TILES - 1)
+        quant_w2()
+        quant_z(0, 0, NPAIR)
         scores_pass(0, *PIECES[0])
         scores_pass(0, *PIECES[1])
         for n, (lo, hi) in enumerate(PIECES):

@@ -18,12 +18,21 @@ ACT = mybir.ActivationFunctionType
 
 P = 128
 PACK = 4
-BANK = 512
 PASS = P * PACK
+RUN = 4
+BANK = 512
 PASSES = H // PASS
 TILES = PASSES * PACK
 NT = N // P
+LIST = 16
+SCALE_ROWS = K // 32
+HALF_PAIRS = NPAIR // 2
 PIECES = ((0, 256), (256, 384), (384, 512))
+WA_GROUPS = ((0, 2), (2, 4), (4, 8))
+
+
+def halves(ap):
+    return [ap[:, half * BANK : (half + 1) * BANK] for half in range(2)]
 
 
 def tile_list_sleep_arousal_scores_kernel(
@@ -35,19 +44,24 @@ def tile_list_sleep_arousal_scores_kernel(
         ring = ctx.enter_context(tc.tile_pool(name="ring", bufs=2))
         psum = ctx.enter_context(tc.psum_pool(name="psum", bufs=1))
 
-        offs_sb = keep.tile([P, S // 16], U16, name="offs_sb")
-        pos1_sb = keep.tile([P, NPAIR // 16], U16, name="pos1_sb")
-        pos2_sb = keep.tile([P, NPAIR // 16], U16, name="pos2_sb")
+        offs_sb = keep.tile([P, S // LIST], U16, name="offs_sb")
+        pos1_sb = keep.tile([P, NPAIR // LIST], U16, name="pos1_sb")
+        pos2_sb = keep.tile([P, NPAIR // LIST], U16, name="pos2_sb")
 
         def load_scale_rows(dst, src):
-            nc.sync.dma_start(dst.bitcast(I32), src[0].bitcast(I32).unsqueeze(1).broadcast_to([16, 8, src.shape[2] // 4]))
+            rows = src[0].bitcast(I32).unsqueeze(1)
+            nc.sync.dma_start(dst.bitcast(I32), rows.broadcast_to([SCALE_ROWS, 8, src.shape[2] // 4]))
 
         tabs_sb = keep.tile([P, T], U8, name="tabs_sb", align_bytes=64)
         tabw_sb = keep.tile([P, T], I32, name="tabw_sb", align_bytes=64)
         wbs_raw = keep.tile([P, H], U8, name="wbs_raw", align_bytes=64)
-        wds_raw = keep.tile([P, H], U8, name="wds_raw", align_bytes=64)
+        wds_raw = keep.tile([P, H], U8, name="wds_raw", tag="late_load0", align_bytes=64)
         planes = keep.tile([P, S + 2 * H], U8, name="planes", align_bytes=64)
         nc.vector.memset(planes[:].bitcast(I32), 0)
+
+        warm = keep.tile([P, 2], F32, name="warm")
+        nc.gpsimd.memset(warm[:, 0:1], 0.0)
+        nc.scalar.activation(warm[:, 1:2], warm[:, 0:1], ACT.Sigmoid)
 
         load_scale_rows(tabs_sb[:], tab_scales)
         nc.sync.dma_start(offs_sb[:], offs)
@@ -57,7 +71,7 @@ def tile_list_sleep_arousal_scores_kernel(
 
         wb_rows = wb_words[0].bitcast(I32)
         wd_rows = wd_words[0].rearrange("p c i -> p (c i)").bitcast(I32)
-        wa_rows = wa.rearrange("(p j) c -> p j c", j=PACK)
+        wa_rows = wa.rearrange("(p i) c -> p i c", i=PACK)
         wb_raw, wd_raw, wa_raw, wb, wd = {}, {}, {}, {}, {}
 
         def load_packed(b):
@@ -66,64 +80,67 @@ def tile_list_sleep_arousal_scores_kernel(
             wd_raw[b] = keep.tile([P, PASS], I32, name="wd_raw", tag="wd_raw")
             nc.sync.dma_start(wd_raw[b][:], wd_rows[:, b * PASS : (b + 1) * PASS])
 
-        def load_wa(b):
-            wa_raw[b] = keep.tile([P, PACK, PASS], F32, name="wa_raw", tag=("wa_raw", "early0")[b], align_bytes=64)
-            nc.sync.dma_start(wa_raw[b][:], wa_rows[:, :, b * PASS : (b + 1) * PASS])
+        def load_wa(b, tag, queue):
+            wa_raw[b] = keep.tile([P, PACK, PASS], F32, name="wa_raw", tag=tag, align_bytes=64)
+            queue.dma_start(wa_raw[b][:], wa_rows[:, :, b * PASS : (b + 1) * PASS])
 
         def deal_packed(b):
             wb[b] = keep.tile([P, 2 * PASS], U8, name="wb%d" % b, align_bytes=64)
             nc.vector.tensor_copy(
-                wb[b][:].bitcast(I32).rearrange("p (t u i) -> p u t i", t=PACK, i=2),
-                wb_raw[b][:].rearrange("p (u t i) -> p u t i", t=PACK, i=2),
+                wb[b][:].bitcast(I32).rearrange("p (t u w) -> p u t w", t=PACK, w=RUN // 2),
+                wb_raw[b][:].rearrange("p (u t w) -> p u t w", t=PACK, w=RUN // 2),
             )
             wd[b] = keep.tile([P, PASS], I32, name="wd%d" % b, align_bytes=64)
             nc.vector.tensor_copy(
-                wd[b][:].rearrange("p (t u i) -> p u t i", t=PACK, i=4),
-                wd_raw[b][:].rearrange("p (u t i) -> p u t i", t=PACK, i=4),
+                wd[b][:].rearrange("p (t u w) -> p u t w", t=PACK, w=RUN),
+                wd_raw[b][:].rearrange("p (u t w) -> p u t w", t=PACK, w=RUN),
             )
 
         load_packed(0)
-        load_wa(0)
         nc.sync.dma_start(pos1_sb[:], pos1)
         nc.sync.dma_start(pos2_sb[:], pos2)
         theta_sb = keep.tile([P, NT], F32, name="theta_sb")
-        with nc.allow_non_contiguous_dma(reason="one threshold a partition"):
+        with nc.allow_non_contiguous_dma(reason="one threshold a partition and output tile"):
             nc.gpsimd.dma_start(theta_sb[:], theta.rearrange("(c p) -> p c", p=P))
         neg_theta = keep.tile([P, NT], F32, name="neg_theta")
         nc.gpsimd.tensor_scalar(neg_theta[:], theta_sb[:], -1.0, 0.0, ALU.mult, ALU.add)
 
         vs_picked = keep.tile([P, S], U8, name="vs_picked", align_bytes=64)
         nc.vector.tensor_copy(vs_picked[:], tabs_sb[:].indirect(offs_sb[:]))
-        staged = keep.tile([P, (S + 2 * H) // 4], I32, name="staged", tag="early0", align_bytes=64)
-        for at, raw in ((S // 4, wbs_raw), ((S + H) // 4, wds_raw)):
+        staged = keep.tile([P, (S + 2 * H) // 4], I32, name="staged", tag="late_load1", align_bytes=64)
+
+        def deal_scales(at, raw):
             nc.vector.tensor_copy(
                 staged[:, at : at + H // 4].rearrange("p (b t u) -> p b t u", b=PASSES, t=PACK),
                 raw[:].bitcast(I32).rearrange("p (b u t) -> p b t u", b=PASSES, t=PACK),
             )
-        nc.vector.tensor_copy(staged[:, 0 : S // 4], vs_picked[:].bitcast(I32))
-        for q in range(4):
-            nc.scalar.dma_start(planes[32 * q : 32 * q + 4, :].bitcast(I32), staged[32 * q : 32 * q + 32 : 8, :])
 
-        vw = []
+        deal_scales(S // 4, wbs_raw)
+        nc.vector.tensor_copy(staged[:, 0 : S // 4], vs_picked[:].bitcast(I32))
+        deal_scales((S + H) // 4, wds_raw)
+        for d in range(4):
+            nc.scalar.dma_start(planes[32 * d : 32 * d + 4, :].bitcast(I32), staged[32 * d : 32 * d + 32 : 8, :])
+        load_wa(0, "late_load0", nc.scalar)
+        v_scales = halves(planes)
+
+        v_words = []
 
         def pick_words(half):
-            vw.append(keep.tile([P, BANK], U32, name="vw%d" % half, align_bytes=64))
-            nc.vector.tensor_copy(
-                vw[half][:], tabw_sb[:].bitcast(U32).indirect(offs_sb[:, half * 32 : (half + 1) * 32])
-            )
+            v_words.append(keep.tile([P, BANK], U32, name="v_words%d" % half, align_bytes=64))
+            columns = slice(half * BANK // LIST, (half + 1) * BANK // LIST)
+            nc.vector.tensor_copy(v_words[half][:], tabw_sb[:].bitcast(U32).indirect(offs_sb[:, columns]))
 
-        wa_groups = ((0, 2), (2, 4), (4, 8))
         wa_bf, wa_codes, wa_scales = {}, {}, {}
 
         def cast_wa(j, copy):
             b, t = divmod(j, PACK)
-            lo, hi = [g for g in wa_groups if g[0] <= j < g[1]][0]
+            lo, hi = [group for group in WA_GROUPS if group[0] <= j < group[1]][0]
             if j == lo:
                 wa_bf[lo] = keep.tile([P, (hi - lo) * PASS], BF16, name="wa_bf%d" % lo,
-                                      tag="early1" if j == 0 else "wa_bf%d" % lo, align_bytes=64)
+                                      tag="late_load2" if j == 0 else "wa_bf%d" % lo, align_bytes=64)
             copy(
-                wa_bf[lo][:, (j - lo) * PASS : (j - lo + 1) * PASS].rearrange("p (u i j) -> p u j i", i=4, j=PACK),
-                wa_raw[b][:].rearrange("p j (u t i) -> p t u j i", t=PACK, i=4)[:, t],
+                wa_bf[lo][:, (j - lo) * PASS : (j - lo + 1) * PASS].rearrange("p (u w i) -> p u i w", w=RUN, i=PACK),
+                wa_raw[b][:].rearrange("p i (u t w) -> p t u i w", t=PACK, w=RUN)[:, t],
             )
 
         def quant_wa(lo, hi):
@@ -134,186 +151,195 @@ def tile_list_sleep_arousal_scores_kernel(
                 wa_codes[j] = codes[:, (j - lo) * P : (j - lo + 1) * P]
                 wa_scales[j] = scales[:, (j - lo) * P : (j - lo + 1) * P]
 
-        held = {(3, 0): "wa_codes4", (7, 0): "w2_codes", (7, 1): "z_codes0_0"}
-        b_tiles, bd_tiles, a_tiles, h_tiles = {}, {}, {}, {}
+        code_tags = {3: "wa_codes%d" % PACK, TILES - 1: "late_codes"}
+        first_reuse = 3
+        b_parts, bd_parts, b_whole, bd_whole, a_tiles, h_tiles = {}, {}, {}, {}, {}, {}
 
-        def products(j, *halves):
+        def assign_buffers(j):
+            if j in code_tags:
+                b_parts[j] = [keep.tile([P, BANK], F32, name="b_part", tag=tag, align_bytes=64)[:]
+                              for tag in (code_tags[j], "b_second%d" % j)]
+            else:
+                b_whole[j] = ring.tile([P, S], F32, name="b_sb", tag="b_sb", bufs=4)
+                b_parts[j] = halves(b_whole[j])
+            if j < first_reuse:
+                bd_whole[j] = ring.tile([P, S], F32, name="bd", tag="bd", bufs=first_reuse)
+            elif j - 1 in b_whole:
+                bd_whole[j] = b_whole[j - 1]
+            if j in bd_whole:
+                bd_parts[j] = halves(bd_whole[j])
+            else:
+                bd_first = keep.tile([P, BANK], F32, name="bd_first")
+                bd_parts[j] = [bd_first[:], b_parts[j - 1][1]]
+
+        def first_stage(tag, bufs, codes, scales, half):
+            acc = psum.tile([P, BANK], F32, name=tag, tag=tag, bufs=bufs)
+            nc.tensor.matmul_mx(out=acc[:], lhsT=codes, lhsT_scale=scales, rhs=v_words[half][:].bitcast(FP8X4),
+                                rhs_scale=v_scales[half], start=True, stop=True)
+            return acc
+
+        banks = (("pb", 2), ("pd", 3), ("pa", 3))
+
+        def products(j, half):
             b, t = divmod(j, PACK)
-            for half in halves:
-                rhs = vw[half][:].bitcast(FP8X4)
-                rhs_scale = planes[:, half * BANK : (half + 1) * BANK]
-                pb = psum.tile([P, BANK], F32, name="pb", tag="pb", bufs=2)
-                nc.tensor.matmul_mx(out=pb[:], lhsT=wb[b][:, t * 2 * P : (t + 1) * 2 * P].bitcast(FP4X4),
-                                    lhsT_scale=planes[:, S + j * P : S + (j + 1) * P],
-                                    rhs=rhs, rhs_scale=rhs_scale, start=True, stop=True)
-                pd = psum.tile([P, BANK], F32, name="pd", tag="pd", bufs=3)
-                nc.tensor.matmul_mx(out=pd[:], lhsT=wd[b][:, t * P : (t + 1) * P].bitcast(FP8X4),
-                                    lhsT_scale=planes[:, S + H + j * P : S + H + (j + 1) * P],
-                                    rhs=rhs, rhs_scale=rhs_scale, start=True, stop=True)
-                if (j, half) in held:
-                    b_sb = keep.tile([P, BANK], F32, name="b_held", tag=held[j, half], align_bytes=64)
-                else:
-                    b_sb = ring.tile([P, BANK], F32, name="b_sb", tag="b_sb", bufs=8)
-                b_tiles[j, half] = b_sb
-                nc.scalar.copy(b_sb[:], pb[:])
-                if j < 3 or (j, half) == (4, 0):
-                    bd = ring.tile([P, BANK], F32, name="bd", tag="bd", bufs=6)
-                else:
-                    bd = b_tiles[j - 1, half]
-                bd_tiles[j, half] = bd
-                nc.vector.tensor_tensor(bd[:], pd[:], b_sb[:], ALU.mult)
+            if half == 0:
+                assign_buffers(j)
+            pb = first_stage(*banks[0], wb[b][:, t * 2 * P : (t + 1) * 2 * P].bitcast(FP4X4),
+                             planes[:, S + j * P : S + (j + 1) * P], half)
+            pd = first_stage(*banks[1], wd[b][:, t * P : (t + 1) * P].bitcast(FP8X4),
+                             planes[:, S + H + j * P : S + H + (j + 1) * P], half)
+            nc.scalar.copy(b_parts[j][half], pb[:])
+            nc.vector.tensor_tensor(bd_parts[j][half], pd[:], b_parts[j][half], ALU.mult)
 
         def linear(j, half):
-            pa = psum.tile([P, BANK], F32, name="pa", tag="pa", bufs=3)
-            nc.tensor.matmul_mx(out=pa[:], lhsT=wa_codes[j].bitcast(FP8X4), lhsT_scale=wa_scales[j],
-                                rhs=vw[half][:].bitcast(FP8X4), rhs_scale=planes[:, half * BANK : (half + 1) * BANK],
-                                start=True, stop=True)
-            return pa
+            return first_stage(*banks[2], wa_codes[j].bitcast(FP8X4), wa_scales[j], half)
 
-        def linear_first(j):
-            for half in range(2):
-                a_tiles[j, half] = ring.tile([P, BANK], F32, name="a_sb", tag="a_sb", bufs=4)
-                nc.scalar.copy(a_tiles[j, half][:], linear(j, half)[:])
+        def gpsimd_halves(j):
+            return 0 if j == 0 else 1 if j == TILES - 1 else 2
+
+        def linear_to_sbuf(j):
+            a_tiles[j] = ring.tile([P, S], F32, name="a_sb", tag="a_sb", bufs=2)
+            for half in range(gpsimd_halves(j)):
+                nc.scalar.copy(halves(a_tiles[j])[half], linear(j, half)[:])
 
         def join(j):
             h_tiles[j] = ring.tile([P, S], F32, name="h", tag="h", bufs=2)
-            for half in range(2):
-                cols = slice(half * BANK, (half + 1) * BANK)
-                if 0 < j < TILES - 1:
-                    nc.gpsimd.tensor_tensor(h_tiles[j][:, cols], a_tiles[j, half][:], bd_tiles[j, half][:], ALU.add)
+            if gpsimd_halves(j) == 2 and j in bd_whole:
+                nc.gpsimd.tensor_tensor(h_tiles[j][:], a_tiles[j][:], bd_whole[j][:], ALU.add)
+                return
+            for half, h_part in enumerate(halves(h_tiles[j])):
+                if half < gpsimd_halves(j):
+                    nc.gpsimd.tensor_tensor(h_part, halves(a_tiles[j])[half], bd_parts[j][half], ALU.add)
                 else:
-                    nc.vector.tensor_tensor(h_tiles[j][:, cols], linear(j, half)[:], bd_tiles[j, half][:], ALU.add)
+                    nc.vector.tensor_tensor(h_part, linear(j, half)[:], bd_parts[j][half], ALU.add)
 
         z32 = [keep.tile([P, PACK, NPAIR], F32, name="z32_%d" % b) for b in range(PASSES)]
 
-        def pick(j, lo, hi, before):
+        def pick_before(j, lo, hi, before):
+            nc.vector.tensor_copy(before, h_tiles[j][:].indirect(pos2_sb[:, lo // LIST : hi // LIST]))
+
+        def pick_change(j, lo, hi, before):
             b, t = divmod(j, PACK)
-            nc.vector.tensor_copy(before, h_tiles[j][:].indirect(pos2_sb[:, lo // 16 : hi // 16]))
-            return lambda: nc.vector.tensor_tensor(
-                z32[b][:, t, lo:hi], h_tiles[j][:].indirect(pos1_sb[:, lo // 16 : hi // 16]), before, ALU.subtract)
+            nc.vector.tensor_tensor(z32[b][:, t, lo:hi], h_tiles[j][:].indirect(pos1_sb[:, lo // LIST : hi // LIST]),
+                                    before, ALU.subtract)
 
         z_bf = [keep.tile([P, NPAIR * PACK], BF16, name="z_bf%d" % b, align_bytes=64) for b in range(PASSES)]
         z_codes, z_scales = {}, {}
 
-        def cast_z(b, lo, hi, copy):
-            copy(z_bf[b][:, lo * PACK : hi * PACK].rearrange("p (c i t) -> p c t i", i=4, t=PACK),
-                 z32[b][:, :, lo:hi].rearrange("p t (c i) -> p c t i", i=4))
+        def cast_z(b, lo, hi, at, copy):
+            copy(z_bf[b][:, at * PACK : (at + hi - lo) * PACK].rearrange("p (c w t) -> p c t w", w=RUN, t=PACK),
+                 z32[b][:, :, lo:hi].rearrange("p t (c w) -> p c t w", w=RUN))
 
-        def quant_z(b, lo, hi):
-            z_codes[b, lo] = keep.tile([P, hi - lo], U32, name="z_codes%d_%d" % (b, lo), tag="z_codes%d_%d" % (b, lo), align_bytes=64)
+        def quant_z(b, lo, hi, at, codes):
+            z_codes[b, lo] = codes
             z_scales[b, lo] = keep.tile([P, hi - lo], U8, name="z_scales%d_%d" % (b, lo), align_bytes=64)
-            nc.vector.quantize_mx(out=z_codes[b, lo][:].bitcast(FP8X4), scales=z_scales[b, lo][:],
-                                  in_=z_bf[b][:, lo * PACK : hi * PACK])
+            nc.vector.quantize_mx(out=codes.bitcast(FP8X4), scales=z_scales[b, lo][:],
+                                  in_=z_bf[b][:, at * PACK : (at + hi - lo) * PACK])
 
-        w2_rows = w2.rearrange("(b u t i) n -> b t u i n", b=PASSES, t=PACK, i=4)
+        w2_rows = w2.rearrange("(b u t w) n -> b t u w n", b=PASSES, t=PACK, w=RUN)
         w2_raw = {}
 
-        def load_w2(b):
-            w2_raw[b] = keep.tile([P, PACK, N], F32, name="w2_raw", tag=("early1", "wa_raw")[b], align_bytes=64)
+        def load_w2(b, tag):
+            w2_raw[b] = keep.tile([P, PACK, N], F32, name="w2_raw", tag=tag, align_bytes=64)
             for t in range(PACK):
                 nc.sync.dma_start(w2_raw[b][:, t, :], w2_rows[b, t])
 
         w2_bf = keep.tile([P, PASSES * N * PACK], BF16, name="w2_bf", align_bytes=64)
-        w2_codes = []
         w2_scales = keep.tile([P, PASSES * N], U8, name="w2_scales", align_bytes=64)
 
-        def cast_w2(piece):
-            b, c = divmod(piece, NT)
+        def cast_w2(part):
+            b, c = divmod(part, NT)
             nc.scalar.copy(
-                w2_bf[:, piece * PASS : (piece + 1) * PASS].rearrange("p (c i t) -> p c t i", i=4, t=PACK),
-                w2_raw[b][:, :, c * P : (c + 1) * P].rearrange("p t (c i) -> p c t i", i=4),
+                w2_bf[:, part * PASS : (part + 1) * PASS].rearrange("p (c w t) -> p c t w", w=RUN, t=PACK),
+                w2_raw[b][:, :, c * P : (c + 1) * P].rearrange("p t (c w) -> p c t w", w=RUN),
             )
-
-        def quant_w2():
-            w2_codes.append(keep.tile([P, PASSES * N], U32, name="w2_codes", tag="w2_codes", align_bytes=64))
-            for lo, hi in ((0, 512), (512, PASSES * N)):
-                nc.vector.quantize_mx(out=w2_codes[0][:, lo:hi].bitcast(FP8X4), scales=w2_scales[:, lo:hi],
-                                      in_=w2_bf[:, lo * PACK : hi * PACK])
-
-        out_rows = out.rearrange("(c p) m -> p c m", p=P)
-        bank_tags = (("pb", 2), ("pd", 3), ("pa", 3))
-        y_banks = {}
-
-        def scores_pass(b, lo, hi):
-            for c in range(NT):
-                if b == 0:
-                    y_banks[lo, c] = psum.tile([P, hi - lo], F32, name="py", tag=bank_tags[c][0], bufs=bank_tags[c][1])
-                    rhs, rhs_scale = z_codes[0, 0][:, lo:hi], z_scales[0, 0][:, lo:hi]
-                else:
-                    rhs, rhs_scale = z_codes[b, lo][:], z_scales[b, lo][:]
-                cols = slice(b * N + c * P, b * N + (c + 1) * P)
-                nc.tensor.matmul_mx(out=y_banks[lo, c][:], lhsT=w2_codes[0][:, cols].bitcast(FP8X4),
-                                    lhsT_scale=w2_scales[:, cols], rhs=rhs.bitcast(FP8X4), rhs_scale=rhs_scale,
-                                    start=(b == 0), stop=(b == PASSES - 1))
-
-        def finish(lo, hi):
-            res = keep.tile([P, NT, hi - lo], F32, name="res%d" % lo)
-            for c in range(NT):
-                nc.scalar.activation(res[:, c, :], y_banks[lo, c][:], ACT.Sigmoid, bias=neg_theta[:, c : c + 1])
-            nc.sync.dma_start(out_rows[:, :, lo:hi], res[:])
 
         pick_words(0)
         deal_packed(0)
         pick_words(1)
         load_packed(1)
-        load_wa(1)
+        load_wa(1, "late_load1", nc.sync)
         cast_wa(0, nc.vector.tensor_copy)
         cast_wa(1, nc.vector.tensor_copy)
         products(0, 0)
-        quant_wa(0, 2)
-        load_w2(0)
+        quant_wa(*WA_GROUPS[0])
+        load_w2(0, "late_load2")
         products(0, 1)
+        cast_wa(2, nc.scalar.copy)
+        cast_wa(3, nc.scalar.copy)
+        load_w2(1, "late_load0")
         products(1, 0)
         join(0)
+        quant_wa(*WA_GROUPS[1])
         products(1, 1)
-        linear_first(1)
+        linear_to_sbuf(1)
         deal_packed(1)
         for j in range(TILES - 2):
-            products(j + 2, 0)
             join(j + 1)
+            products(j + 2, 0)
             products(j + 2, 1)
-            if j == 0:
-                cast_wa(2, nc.scalar.copy)
-                cast_wa(3, nc.scalar.copy)
-                quant_wa(2, 4)
-                load_w2(1)
-            if j == 1:
-                for t in range(PACK):
-                    cast_wa(PACK + t, nc.scalar.copy)
-            if j + 3 < TILES:
-                linear_first(j + 2)
-            if 2 <= j < 5:
-                cast_w2(j - 2)
-            if j == 5:
-                for piece in range(NT, 2 * NT):
-                    cast_w2(piece)
-                cast_z(0, 0, 256, nc.scalar.copy)
-                cast_z(0, 256, 512, nc.scalar.copy)
-            first_sub = pick(j, 0, 256, b_tiles[j + 2, 0][:, 0:256])
-            second_sub = pick(j, 256, 512, b_tiles[j + 2, 1][:, 0:256])
-            first_sub()
-            second_sub()
-            if j == 1:
-                quant_wa(4, 8)
+            linear_to_sbuf(j + 2)
+            if 2 * j < PACK:
+                cast_wa(PACK + 2 * j, nc.scalar.copy)
+                cast_wa(PACK + 2 * j + 1, nc.scalar.copy)
+            elif 2 * j - PACK < PASSES * NT:
+                cast_w2(2 * j - PACK)
+                cast_w2(2 * j - PACK + 1)
+            if j >= PACK:
+                lo = (j - PACK) * HALF_PAIRS
+                cast_z(0, lo, lo + HALF_PAIRS, lo, nc.scalar.copy)
+            for step in (pick_before, pick_change):
+                for half in range(2):
+                    step(j, half * HALF_PAIRS, (half + 1) * HALF_PAIRS, b_parts[j + 2][half][:, 0:HALF_PAIRS])
+            if j + 2 == min(code_tags):
+                quant_wa(*WA_GROUPS[2])
+
+        late_codes = keep.tile([P, PASSES * N + NPAIR], U32, name="late_codes", tag="late_codes", align_bytes=64)
+        for lo, hi in ((0, PASS), (PASS, PASSES * N)):
+            nc.vector.quantize_mx(out=late_codes[:, lo:hi].bitcast(FP8X4), scales=w2_scales[:, lo:hi],
+                                  in_=w2_bf[:, lo * PACK : hi * PACK])
+        quant_z(0, 0, NPAIR, 0, late_codes[:, PASSES * N :])
         join(TILES - 1)
-        quant_w2()
-        quant_z(0, 0, NPAIR)
+
+        out_rows = out.rearrange("(c p) m -> p c m", p=P)
+        z_last = keep.tile([P, NPAIR], U32, name="z_last", align_bytes=64)
+        y_banks = {}
+
+        def scores_pass(b, lo, hi):
+            for c in range(NT):
+                if b == 0:
+                    y_banks[lo, c] = psum.tile([P, hi - lo], F32, name="py", tag=banks[c][0], bufs=banks[c][1])
+                    rhs, rhs_scale = z_codes[0, 0][:, lo:hi], z_scales[0, 0][:, lo:hi]
+                else:
+                    rhs, rhs_scale = z_codes[b, lo], z_scales[b, lo][:]
+                cols = slice(b * N + c * P, b * N + (c + 1) * P)
+                nc.tensor.matmul_mx(out=y_banks[lo, c][:], lhsT=late_codes[:, cols].bitcast(FP8X4),
+                                    lhsT_scale=w2_scales[:, cols], rhs=rhs.bitcast(FP8X4), rhs_scale=rhs_scale,
+                                    start=(b == 0), stop=(b == PASSES - 1))
+
+        def finish(lo, hi, at):
+            quant_z(1, lo, hi, at, z_last[:, lo:hi])
+            scores_pass(1, lo, hi)
+            res = keep.tile([P, NT, hi - lo], F32, name="res%d" % lo)
+            for c in range(NT):
+                nc.scalar.activation(res[:, c, :], y_banks[lo, c][:], ACT.Sigmoid, bias=neg_theta[:, c : c + 1])
+            nc.sync.dma_start(out_rows[:, :, lo:hi], res[:])
+
+        spare = w2_bf[:].bitcast(F32)[:, PASS * 2 :]
+        before_last = [spare[:, 0:256], spare[:, 256:384], z_bf[1][:].bitcast(F32)[:, 0:128]]
+        before_other = [z_bf[0][:].bitcast(F32)[:, 0:256], before_last[0][:, 0:128], before_last[1]]
         scores_pass(0, *PIECES[0])
         scores_pass(0, *PIECES[1])
         for n, (lo, hi) in enumerate(PIECES):
-            last = n == len(PIECES) - 1
-            before = ring.tile([P, 2, hi - lo], F32, name="before", tag="before", bufs=2)
-            first_sub = pick(TILES - 2, lo, hi, before[:, 0, :])
-            second_sub = pick(TILES - 1, lo, hi, before[:, 1, :])
-            first_sub()
-            second_sub()
+            pick_before(TILES - 2, lo, hi, before_other[n])
+            pick_before(TILES - 1, lo, hi, before_last[n])
+            pick_change(TILES - 2, lo, hi, before_other[n])
+            pick_change(TILES - 1, lo, hi, before_last[n])
             if n > 0:
-                quant_z(1, *PIECES[n - 1])
-                scores_pass(1, *PIECES[n - 1])
-                finish(*PIECES[n - 1])
+                finish(*PIECES[n - 1], PIECES[n - 1][0])
             if n == 1:
                 scores_pass(0, *PIECES[2])
-            cast_z(1, lo, hi, nc.vector.tensor_copy if last else nc.scalar.copy)
-        quant_z(1, lo, hi)
-        scores_pass(1, lo, hi)
-        finish(lo, hi)
+            if n + 1 < len(PIECES):
+                cast_z(1, lo, hi, lo, nc.scalar.copy)
+        cast_z(1, lo, hi, PIECES[1][0], nc.vector.tensor_copy)
+        finish(lo, hi, PIECES[1][0])

@@ -69,34 +69,26 @@ def tile_list_sleep_arousal_scores_kernel(
         load_scale_rows(wds_raw[:], wd_scales)
         nc.sync.dma_start(tabw_sb[:], tab_words[0].rearrange("p t i -> p (t i)").bitcast(I32))
 
-        wb_rows = wb_words[0].bitcast(I32)
-        wd_rows = wd_words[0].rearrange("p c i -> p (c i)").bitcast(I32)
-        wa_rows = wa.rearrange("(p i) c -> p i c", i=PACK)
-        wb_raw, wd_raw, wa_raw, wb, wd = {}, {}, {}, {}, {}
+        wb_raw = keep.tile([P, H // 2], I32, name="wb_raw")
+        nc.sync.dma_start(wb_raw[:], wb_words[0].bitcast(I32))
+        wd_raw = keep.tile([P, H], I32, name="wd_raw")
+        nc.sync.dma_start(wd_raw[:], wd_words[0].rearrange("p c i -> p (c i)").bitcast(I32))
+        wb = keep.tile([P, 2 * H], U8, name="wb", align_bytes=64)
+        wd = keep.tile([P, H], I32, name="wd", align_bytes=64)
 
-        def load_packed(b):
-            wb_raw[b] = keep.tile([P, PASS // 2], I32, name="wb_raw", tag="wb_raw")
-            nc.sync.dma_start(wb_raw[b][:], wb_rows[:, b * PASS // 2 : (b + 1) * PASS // 2])
-            wd_raw[b] = keep.tile([P, PASS], I32, name="wd_raw", tag="wd_raw")
-            nc.sync.dma_start(wd_raw[b][:], wd_rows[:, b * PASS : (b + 1) * PASS])
+        def deal_words(dealt, raw, run_words):
+            nc.vector.tensor_copy(
+                dealt.rearrange("p (b t u w) -> p b u t w", b=PASSES, t=PACK, w=run_words),
+                raw.rearrange("p (b u t w) -> p b u t w", b=PASSES, t=PACK, w=run_words),
+            )
+
+        wa_rows = wa.rearrange("(p i) c -> p i c", i=PACK)
+        wa_raw = {}
 
         def load_wa(b, tag, queue):
             wa_raw[b] = keep.tile([P, PACK, PASS], F32, name="wa_raw", tag=tag, align_bytes=64)
             queue.dma_start(wa_raw[b][:], wa_rows[:, :, b * PASS : (b + 1) * PASS])
 
-        def deal_packed(b):
-            wb[b] = keep.tile([P, 2 * PASS], U8, name="wb%d" % b, align_bytes=64)
-            nc.vector.tensor_copy(
-                wb[b][:].bitcast(I32).rearrange("p (t u w) -> p u t w", t=PACK, w=RUN // 2),
-                wb_raw[b][:].rearrange("p (u t w) -> p u t w", t=PACK, w=RUN // 2),
-            )
-            wd[b] = keep.tile([P, PASS], I32, name="wd%d" % b, align_bytes=64)
-            nc.vector.tensor_copy(
-                wd[b][:].rearrange("p (t u w) -> p u t w", t=PACK, w=RUN),
-                wd_raw[b][:].rearrange("p (u t w) -> p u t w", t=PACK, w=RUN),
-            )
-
-        load_packed(0)
         nc.sync.dma_start(pos1_sb[:], pos1)
         nc.sync.dma_start(pos2_sb[:], pos2)
         theta_sb = keep.tile([P, NT], F32, name="theta_sb")
@@ -181,12 +173,11 @@ def tile_list_sleep_arousal_scores_kernel(
         banks = (("pb", 2), ("pd", 3), ("pa", 3))
 
         def products(j, half):
-            b, t = divmod(j, PACK)
             if half == 0:
                 assign_buffers(j)
-            pb = first_stage(*banks[0], wb[b][:, t * 2 * P : (t + 1) * 2 * P].bitcast(FP4X4),
+            pb = first_stage(*banks[0], wb[:, j * 2 * P : (j + 1) * 2 * P].bitcast(FP4X4),
                              planes[:, S + j * P : S + (j + 1) * P], half)
-            pd = first_stage(*banks[1], wd[b][:, t * P : (t + 1) * P].bitcast(FP8X4),
+            pd = first_stage(*banks[1], wd[:, j * P : (j + 1) * P].bitcast(FP8X4),
                              planes[:, S + H + j * P : S + H + (j + 1) * P], half)
             nc.scalar.copy(b_parts[j][half], pb[:])
             nc.vector.tensor_tensor(bd_parts[j][half], pd[:], b_parts[j][half], ALU.mult)
@@ -255,9 +246,9 @@ def tile_list_sleep_arousal_scores_kernel(
             )
 
         pick_words(0)
-        deal_packed(0)
+        deal_words(wb[:].bitcast(I32), wb_raw[:], RUN // 2)
+        deal_words(wd[:], wd_raw[:], RUN)
         pick_words(1)
-        load_packed(1)
         load_wa(1, "late_load1", nc.sync)
         cast_wa(0, nc.vector.tensor_copy)
         cast_wa(1, nc.vector.tensor_copy)
@@ -273,7 +264,6 @@ def tile_list_sleep_arousal_scores_kernel(
         quant_wa(*WA_GROUPS[1])
         products(1, 1)
         linear_to_sbuf(1)
-        deal_packed(1)
         for j in range(TILES - 2):
             join(j + 1)
             products(j + 2, 0)
@@ -301,7 +291,6 @@ def tile_list_sleep_arousal_scores_kernel(
         quant_z(0, 0, NPAIR, 0, late_codes[:, PASSES * N :])
         join(TILES - 1)
 
-        out_rows = out.rearrange("(c p) m -> p c m", p=P)
         z_last = keep.tile([P, NPAIR], U32, name="z_last", align_bytes=64)
         y_banks = {}
 
@@ -323,7 +312,7 @@ def tile_list_sleep_arousal_scores_kernel(
             res = keep.tile([P, NT, hi - lo], F32, name="res%d" % lo)
             for c in range(NT):
                 nc.scalar.activation(res[:, c, :], y_banks[lo, c][:], ACT.Sigmoid, bias=neg_theta[:, c : c + 1])
-            nc.sync.dma_start(out_rows[:, :, lo:hi], res[:])
+                nc.sync.dma_start(out[c * P : (c + 1) * P, lo:hi], res[:, c, :])
 
         spare = w2_bf[:].bitcast(F32)[:, PASS * 2 :]
         before_last = [spare[:, 0:256], spare[:, 256:384], z_bf[1][:].bitcast(F32)[:, 0:128]]

from contextlib import ExitStack

import concourse.mybir as mybir

K, T, S, NPAIR, H, N = 512, 2048, 1024, 512, 1024, 384
FLOPS = 3 * 2 * K * H * S + 2 * H * N * NPAIR

F32 = mybir.dt.float32
BF16 = mybir.dt.bfloat16
I32 = mybir.dt.int32
U32 = mybir.dt.uint32
U16 = mybir.dt.uint16
U8 = mybir.dt.uint8
FP8X4 = mybir.dt.float8_e4m3fn_x4
FP4X4 = mybir.dt.float4_e2m1fn_x4
ALU = mybir.AluOpType
ACT = mybir.ActivationFunctionType

P = 128
PACK = 4
PASS = P * PACK
RUN = 4
BANK = 512
PASSES = H // PASS
TILES = PASSES * PACK
NT = N // P
LIST = 16
SCALE_ROWS = K // 32
HALF_PAIRS = NPAIR // 2
PIECES = ((0, 256), (256, 384), (384, 512))
WA_GROUPS = ((0, 2), (2, 4), (4, 8))


def halves(ap):
    return [ap[:, half * BANK : (half + 1) * BANK] for half in range(2)]


def tile_list_sleep_arousal_scores_kernel(
    tc, tab_words, tab_scales, offs, wa, wb_words, wb_scales, wd_words, wd_scales, pos1, pos2, w2, theta, out
):
    nc = tc.nc
    with ExitStack() as ctx:
        keep = ctx.enter_context(tc.tile_pool(name="keep", bufs=1))
        ring = ctx.enter_context(tc.tile_pool(name="ring", bufs=2))
        psum = ctx.enter_context(tc.psum_pool(name="psum", bufs=1))

        offs_sb = keep.tile([P, S // LIST], U16, name="offs_sb")
        pos1_sb = keep.tile([P, NPAIR // LIST], U16, name="pos1_sb")
        pos2_sb = keep.tile([P, NPAIR // LIST], U16, name="pos2_sb")

        def load_scale_rows(dst, src):
            rows = src[0].bitcast(I32).unsqueeze(1)
            nc.sync.dma_start(dst.bitcast(I32), rows.broadcast_to([SCALE_ROWS, 8, src.shape[2] // 4]))

        tabs_sb = keep.tile([P, T], U8, name="tabs_sb", align_bytes=64)
        tabw_sb = keep.tile([P, T], I32, name="tabw_sb", align_bytes=64)
        wbs_raw = keep.tile([P, H], U8, name="wbs_raw", align_bytes=64)
        wds_raw = keep.tile([P, H], U8, name="wds_raw", tag="late_load0", align_bytes=64)
        planes = keep.tile([P, S + 2 * H], U8, name="planes", align_bytes=64)
        nc.vector.memset(planes[:].bitcast(I32), 0)

        warm = keep.tile([P, 2], F32, name="warm")
        nc.gpsimd.memset(warm[:, 0:1], 0.0)
        nc.scalar.activation(warm[:, 1:2], warm[:, 0:1], ACT.Sigmoid)

        load_scale_rows(tabs_sb[:], tab_scales)
        nc.sync.dma_start(offs_sb[:], offs)
        load_scale_rows(wbs_raw[:], wb_scales)
        load_scale_rows(wds_raw[:], wd_scales)
        nc.sync.dma_start(tabw_sb[:], tab_words[0].rearrange("p t i -> p (t i)").bitcast(I32))

        wb_raw = keep.tile([P, H // 2], I32, name="wb_raw")
        nc.sync.dma_start(wb_raw[:], wb_words[0].bitcast(I32))
        wd_raw = keep.tile([P, H], I32, name="wd_raw")
        nc.sync.dma_start(wd_raw[:], wd_words[0].rearrange("p c i -> p (c i)").bitcast(I32))
        wb = keep.tile([P, 2 * H], U8, name="wb", align_bytes=64)
        wd = keep.tile([P, H], I32, name="wd", align_bytes=64)

        def deal_words(dealt, raw, run_words):
            nc.vector.tensor_copy(
                dealt.rearrange("p (b t u w) -> p b u t w", b=PASSES, t=PACK, w=run_words),
                raw.rearrange("p (b u t w) -> p b u t w", b=PASSES, t=PACK, w=run_words),
            )

        wa_rows = wa.rearrange("(p i) c -> p i c", i=PACK)
        wa_raw = {}

        def load_wa(b, tag, queue):
            wa_raw[b] = keep.tile([P, PACK, PASS], F32, name="wa_raw", tag=tag, align_bytes=64)
            queue.dma_start(wa_raw[b][:], wa_rows[:, :, b * PASS : (b + 1) * PASS])

        nc.sync.dma_start(pos1_sb[:], pos1)
        nc.sync.dma_start(pos2_sb[:], pos2)
        theta_sb = keep.tile([P, NT], F32, name="theta_sb")
        with nc.allow_non_contiguous_dma(reason="one threshold a partition and output tile"):
            nc.gpsimd.dma_start(theta_sb[:], theta.rearrange("(c p) -> p c", p=P))
        neg_theta = keep.tile([P, NT], F32, name="neg_theta")
        nc.gpsimd.tensor_scalar(neg_theta[:], theta_sb[:], -1.0, 0.0, ALU.mult, ALU.add)

        vs_picked = keep.tile([P, S], U8, name="vs_picked", align_bytes=64)
        nc.vector.tensor_copy(vs_picked[:], tabs_sb[:].indirect(offs_sb[:]))
        staged = keep.tile([P, (S + 2 * H) // 4], I32, name="staged", tag="late_load1", align_bytes=64)

        def deal_scales(at, raw):
            nc.vector.tensor_copy(
                staged[:, at : at + H // 4].rearrange("p (b t u) -> p b t u", b=PASSES, t=PACK),
                raw[:].bitcast(I32).rearrange("p (b u t) -> p b t u", b=PASSES, t=PACK),
            )

        deal_scales(S // 4, wbs_raw)
        nc.vector.tensor_copy(staged[:, 0 : S // 4], vs_picked[:].bitcast(I32))
        deal_scales((S + H) // 4, wds_raw)
        for d in range(4):
            nc.scalar.dma_start(planes[32 * d : 32 * d + 4, :].bitcast(I32), staged[32 * d : 32 * d + 32 : 8, :])
        load_wa(0, "late_load0", nc.scalar)
        v_scales = halves(planes)

        v_words = []

        def pick_words(half):
            v_words.append(keep.tile([P, BANK], U32, name="v_words%d" % half, align_bytes=64))
            columns = slice(half * BANK // LIST, (half + 1) * BANK // LIST)
            nc.vector.tensor_copy(v_words[half][:], tabw_sb[:].bitcast(U32).indirect(offs_sb[:, columns]))

        wa_bf, wa_codes, wa_scales = {}, {}, {}

        def cast_wa(j, copy):
            b, t = divmod(j, PACK)
            lo, hi = [group for group in WA_GROUPS if group[0] <= j < group[1]][0]
            if j == lo:
                wa_bf[lo] = keep.tile([P, (hi - lo) * PASS], BF16, name="wa_bf%d" % lo,
                                      tag="late_load2" if j == 0 else "wa_bf%d" % lo, align_bytes=64)
            copy(
                wa_bf[lo][:, (j - lo) * PASS : (j - lo + 1) * PASS].rearrange("p (u w i) -> p u i w", w=RUN, i=PACK),
                wa_raw[b][:].rearrange("p i (u t w) -> p t u i w", t=PACK, w=RUN)[:, t],
            )

        def quant_wa(lo, hi):
            codes = keep.tile([P, (hi - lo) * P], U32, name="wa_codes%d" % lo, tag="wa_codes%d" % lo, align_bytes=64)
            scales = keep.tile([P, (hi - lo) * P], U8, name="wa_scales%d" % lo, align_bytes=64)
            nc.vector.quantize_mx(out=codes[:].bitcast(FP8X4), scales=scales[:], in_=wa_bf[lo][:])
            for j in range(lo, hi):
                wa_codes[j] = codes[:, (j - lo) * P : (j - lo + 1) * P]
                wa_scales[j] = scales[:, (j - lo) * P : (j - lo + 1) * P]

        code_tags = {3: "wa_codes%d" % PACK, TILES - 1: "late_codes"}
        first_reuse = 3
        b_parts, bd_parts, b_whole, bd_whole, a_tiles, h_tiles = {}, {}, {}, {}, {}, {}

        def assign_buffers(j):
            if j in code_tags:
                b_parts[j] = [keep.tile([P, BANK], F32, name="b_part", tag=tag, align_bytes=64)[:]
                              for tag in (code_tags[j], "b_second%d" % j)]
            else:
                b_whole[j] = ring.tile([P, S], F32, name="b_sb", tag="b_sb", bufs=4)
                b_parts[j] = halves(b_whole[j])
            if j < first_reuse:
                bd_whole[j] = ring.tile([P, S], F32, name="bd", tag="bd", bufs=first_reuse)
            elif j - 1 in b_whole:
                bd_whole[j] = b_whole[j - 1]
            if j in bd_whole:
                bd_parts[j] = halves(bd_whole[j])
            else:
                bd_first = keep.tile([P, BANK], F32, name="bd_first")
                bd_parts[j] = [bd_first[:], b_parts[j - 1][1]]

        def first_stage(tag, bufs, codes, scales, half):
            acc = psum.tile([P, BANK], F32, name=tag, tag=tag, bufs=bufs)
            nc.tensor.matmul_mx(out=acc[:], lhsT=codes, lhsT_scale=scales, rhs=v_words[half][:].bitcast(FP8X4),
                                rhs_scale=v_scales[half], start=True, stop=True)
            return acc

        banks = (("pb", 2), ("pd", 3), ("pa", 3))

        def products(j, half):
            if half == 0:
                assign_buffers(j)
            pb = first_stage(*banks[0], wb[:, j * 2 * P : (j + 1) * 2 * P].bitcast(FP4X4),
                             planes[:, S + j * P : S + (j + 1) * P], half)
            pd = first_stage(*banks[1], wd[:, j * P : (j + 1) * P].bitcast(FP8X4),
                             planes[:, S + H + j * P : S + H + (j + 1) * P], half)
            nc.scalar.copy(b_parts[j][half], pb[:])
            nc.vector.tensor_tensor(bd_parts[j][half], pd[:], b_parts[j][half], ALU.mult)

        def linear(j, half):
            return first_stage(*banks[2], wa_codes[j].bitcast(FP8X4), wa_scales[j], half)

        def gpsimd_halves(j):
            return 0 if j == 0 else 1 if j == TILES - 1 else 2

        def linear_to_sbuf(j):
            a_tiles[j] = ring.tile([P, S], F32, name="a_sb", tag="a_sb", bufs=2)
            for half in range(gpsimd_halves(j)):
                nc.scalar.copy(halves(a_tiles[j])[half], linear(j, half)[:])

        def join(j):
            h_tiles[j] = ring.tile([P, S], F32, name="h", tag="h", bufs=2)
            if gpsimd_halves(j) == 2 and j in bd_whole:
                nc.gpsimd.tensor_tensor(h_tiles[j][:], a_tiles[j][:], bd_whole[j][:], ALU.add)
                return
            for half, h_part in enumerate(halves(h_tiles[j])):
                if half < gpsimd_halves(j):
                    nc.gpsimd.tensor_tensor(h_part, halves(a_tiles[j])[half], bd_parts[j][half], ALU.add)
                else:
                    nc.vector.tensor_tensor(h_part, linear(j, half)[:], bd_parts[j][half], ALU.add)

        z32 = [keep.tile([P, PACK, NPAIR], F32, name="z32_%d" % b) for b in range(PASSES)]

        def pick_before(j, lo, hi, before):
            nc.vector.tensor_copy(before, h_tiles[j][:].indirect(pos2_sb[:, lo // LIST : hi // LIST]))

        def pick_change(j, lo, hi, before):
            b, t = divmod(j, PACK)
            nc.vector.tensor_tensor(z32[b][:, t, lo:hi], h_tiles[j][:].indirect(pos1_sb[:, lo // LIST : hi // LIST]),
                                    before, ALU.subtract)

        z_bf = [keep.tile([P, NPAIR * PACK], BF16, name="z_bf%d" % b, align_bytes=64) for b in range(PASSES)]
        z_codes, z_scales = {}, {}

        def cast_z(b, lo, hi, at, copy):
            copy(z_bf[b][:, at * PACK : (at + hi - lo) * PACK].rearrange("p (c w t) -> p c t w", w=RUN, t=PACK),
                 z32[b][:, :, lo:hi].rearrange("p t (c w) -> p c t w", w=RUN))

        def quant_z(b, lo, hi, at, codes):
            z_codes[b, lo] = codes
            z_scales[b, lo] = keep.tile([P, hi - lo], U8, name="z_scales%d_%d" % (b, lo), align_bytes=64)
            nc.vector.quantize_mx(out=codes.bitcast(FP8X4), scales=z_scales[b, lo][:],
                                  in_=z_bf[b][:, at * PACK : (at + hi - lo) * PACK])

        w2_rows = w2.rearrange("(b u t w) n -> b t u w n", b=PASSES, t=PACK, w=RUN)
        w2_raw = {}

        def load_w2(b, tag):
            w2_raw[b] = keep.tile([P, PACK, N], F32, name="w2_raw", tag=tag, align_bytes=64)
            for t in range(PACK):
                nc.sync.dma_start(w2_raw[b][:, t, :], w2_rows[b, t])

        w2_bf = keep.tile([P, PASSES * N * PACK], BF16, name="w2_bf", align_bytes=64)
        w2_scales = keep.tile([P, PASSES * N], U8, name="w2_scales", align_bytes=64)

        def cast_w2(part):
            b, c = divmod(part, NT)
            nc.scalar.copy(
                w2_bf[:, part * PASS : (part + 1) * PASS].rearrange("p (c w t) -> p c t w", w=RUN, t=PACK),
                w2_raw[b][:, :, c * P : (c + 1) * P].rearrange("p t (c w) -> p c t w", w=RUN),
            )

        pick_words(0)
        deal_words(wb[:].bitcast(I32), wb_raw[:], RUN // 2)
        deal_words(wd[:], wd_raw[:], RUN)
        pick_words(1)
        load_wa(1, "late_load1", nc.sync)
        cast_wa(0, nc.vector.tensor_copy)
        cast_wa(1, nc.vector.tensor_copy)
        products(0, 0)
        quant_wa(*WA_GROUPS[0])
        load_w2(0, "late_load2")
        products(0, 1)
        cast_wa(2, nc.scalar.copy)
        cast_wa(3, nc.scalar.copy)
        load_w2(1, "late_load0")
        products(1, 0)
        join(0)
        quant_wa(*WA_GROUPS[1])
        products(1, 1)
        linear_to_sbuf(1)
        for j in range(TILES - 2):
            join(j + 1)
            products(j + 2, 0)
            products(j + 2, 1)
            linear_to_sbuf(j + 2)
            if 2 * j < PACK:
                cast_wa(PACK + 2 * j, nc.scalar.copy)
                cast_wa(PACK + 2 * j + 1, nc.scalar.copy)
            elif 2 * j - PACK < PASSES * NT:
                cast_w2(2 * j - PACK)
                cast_w2(2 * j - PACK + 1)
            if j >= PACK:
                lo = (j - PACK) * HALF_PAIRS
                cast_z(0, lo, lo + HALF_PAIRS, lo, nc.scalar.copy)
            for step in (pick_before, pick_change):
                for half in range(2):
                    step(j, half * HALF_PAIRS, (half + 1) * HALF_PAIRS, b_parts[j + 2][half][:, 0:HALF_PAIRS])
            if j + 2 == min(code_tags):
                quant_wa(*WA_GROUPS[2])

        late_codes = keep.tile([P, PASSES * N + NPAIR], U32, name="late_codes", tag="late_codes", align_bytes=64)
        for lo, hi in ((0, PASS), (PASS, PASSES * N)):
            nc.vector.quantize_mx(out=late_codes[:, lo:hi].bitcast(FP8X4), scales=w2_scales[:, lo:hi],
                                  in_=w2_bf[:, lo * PACK : hi * PACK])
        quant_z(0, 0, NPAIR, 0, late_codes[:, PASSES * N :])
        join(TILES - 1)

        z_last = keep.tile([P, NPAIR], U32, name="z_last", align_bytes=64)
        y_banks = {}

        def scores_pass(b, lo, hi):
            for c in range(NT):
                if b == 0:
                    y_banks[lo, c] = psum.tile([P, hi - lo], F32, name="py", tag=banks[c][0], bufs=banks[c][1])
                    rhs, rhs_scale = z_codes[0, 0][:, lo:hi], z_scales[0, 0][:, lo:hi]
                else:
                    rhs, rhs_scale = z_codes[b, lo], z_scales[b, lo][:]
                cols = slice(b * N + c * P, b * N + (c + 1) * P)
                nc.tensor.matmul_mx(out=y_banks[lo, c][:], lhsT=late_codes[:, cols].bitcast(FP8X4),
                                    lhsT_scale=w2_scales[:, cols], rhs=rhs.bitcast(FP8X4), rhs_scale=rhs_scale,
                                    start=(b == 0), stop=(b == PASSES - 1))

        def finish(lo, hi, at):
            quant_z(1, lo, hi, at, z_last[:, lo:hi])
            scores_pass(1, lo, hi)
            res = keep.tile([P, NT, hi - lo], F32, name="res%d" % lo)
            for c in range(NT):
                nc.scalar.activation(res[:, c, :], y_banks[lo, c][:], ACT.Sigmoid, bias=neg_theta[:, c : c + 1])
                nc.sync.dma_start(out[c * P : (c + 1) * P, lo:hi], res[:, c, :])

        spare = w2_bf[:].bitcast(F32)[:, PASS * 2 :]
        before_last = [spare[:, 0:256], spare[:, 256:384], z_bf[1][:].bitcast(F32)[:, 0:128]]
        before_other = [z_bf[0][:].bitcast(F32)[:, 0:256], before_last[0][:, 0:128], before_last[1]]
        scores_pass(0, *PIECES[0])
        scores_pass(0, *PIECES[1])
        for n, (lo, hi) in enumerate(PIECES):
            pick_before(TILES - 2, lo, hi, before_other[n])
            pick_before(TILES - 1, lo, hi, before_last[n])
            pick_change(TILES - 2, lo, hi, before_other[n])
            pick_change(TILES - 1, lo, hi, before_last[n])
            if n > 0:
                finish(*PIECES[n - 1], PIECES[n - 1][0])
            if n == 1:
                scores_pass(0, *PIECES[2])
            if n + 1 < len(PIECES):
                cast_z(1, lo, hi, lo, nc.scalar.copy)
        cast_z(1, lo, hi, PIECES[1][0], nc.vector.tensor_copy)
        finish(lo, hi, PIECES[1][0])
